import numpy as np
import ml_dtypes


def mxq(x, axis, fmt="e4m3"):
    dtype, down = {"e4m3": (ml_dtypes.float8_e4m3fn, 7), "e5m2": (ml_dtypes.float8_e5m2, 14)}[fmt]
    v = np.moveaxis(np.asarray(x, np.float32).astype(ml_dtypes.bfloat16).astype(np.float64), axis, -1)
    blocks = v.reshape(v.shape[:-1] + (-1, 32))
    amax = np.abs(blocks).max(-1, keepdims=True)
    byte = np.maximum(np.where(amax > 0, np.frexp(amax)[1] - 1 + 127, 0) - down, 1)
    scale = np.exp2(byte - 127.0)
    codes = (blocks / scale).astype(np.float32).astype(dtype).astype(np.float64)
    return np.moveaxis((codes * scale).reshape(v.shape), -1, axis)


WIDE = False


def mx_kscale(k):
    if not WIDE:
        return np.ones(k)
    levels = np.array([24, -24, 12, -12, 0])
    if k % 512:
        return np.exp2(np.random.permutation(np.resize(levels, k // 32))).repeat(32)
    a = np.empty((k // 512, 16))
    for p in range(k // 512):
        a[p, :8] = np.random.permutation(np.resize(levels, 8))
        for g in range(8):
            far = levels[np.abs(levels - a[p, g]) >= 10]
            a[p, g + 8] = far[np.random.randint(len(far))]
    return np.exp2(a.ravel()).repeat(32)


def f64(x):
    return np.asarray(x).astype(np.float64)


def striped(idx):
    return np.tile(idx.reshape(-1, 16).T, (8, 1)).astype(np.uint16)


def unstriped(offs):
    return offs[:16].T.reshape(-1).astype(np.int64)


E2M1 = np.array([0.0, 0.5, 1.0, 1.5, 2.0, 3.0, 4.0, 6.0, -0.0, -0.5, -1.0, -1.5, -2.0, -3.0, -4.0, -6.0])


def pack_weight(w, fmt):
    k, n = w.shape
    w = f64(np.asarray(w, np.float32).astype(ml_dtypes.bfloat16)).reshape(k // 32, 32, n)
    amax = np.abs(w).max(1)
    if fmt == "e4m3":
        byte = np.frexp(amax)[1] - 1 + 127 - 7
    else:
        mant, ex = np.frexp(amax / 6.0)
        byte = np.where(mant > 0.5, ex, ex - 1) + 127
    byte = np.clip(np.where(amax > 0, byte, 1), 1, 254)
    scaled = (w * np.exp2(127.0 - byte)[:, None, :]).reshape(k, n).astype(np.float32)
    by_word = np.ascontiguousarray(scaled.reshape(k // 512, 128, 4, n).transpose(0, 1, 3, 2))
    if fmt == "e4m3":
        words = by_word.astype(ml_dtypes.float8_e4m3fn).view(np.uint8)
    else:
        c = by_word.astype(ml_dtypes.float4_e2m1fn).view(np.uint8) & 0xF
        words = (c[..., 0::2] | (c[..., 1::2] << 4)).reshape(k // 512, 128, 2 * n)
    return np.ascontiguousarray(words), np.ascontiguousarray(byte.astype(np.uint8).reshape(k // 512, 16, n))


def unpack_weight(words, scales, fmt):
    g, _, n = scales.shape
    words = np.ascontiguousarray(words).reshape(g, 128, n, -1)
    if fmt == "e4m3":
        vals = words.view(ml_dtypes.float8_e4m3fn).astype(np.float64)
    else:
        nib = np.empty((g, 128, n, 4), np.uint8)
        nib[..., 0::2] = words & 0xF
        nib[..., 1::2] = words >> 4
        vals = E2M1[nib]
    vals = vals * np.repeat(np.exp2(scales.astype(np.float64) - 127.0), 8, axis=1)[..., None]
    return vals.transpose(0, 1, 3, 2).reshape(g * 512, n)


def pack_table4(v):
    words, scales = pack_weight(v, "e2m1")
    g, t = words.shape[0] // 2, v.shape[1]
    return np.ascontiguousarray(words.reshape(g, 2, 128, t, 2).transpose(0, 2, 3, 1, 4).reshape(g, 128, t, 4)), scales


def unpack_table4(words, scales):
    g, _, t, _ = words.shape
    return unpack_weight(words.reshape(g, 128, t, 2, 2).transpose(0, 3, 1, 2, 4).reshape(2 * g, 128, 2 * t), scales, "e2m1")


K, L, N, T, J = 1024, 1024, 512, 2048, 512


def setup_inputs():
    n = np.random.standard_normal
    s = mx_kscale(K)[:, None]
    s2 = mx_kscale(L)[:, None]
    p_tab = pack_table4(n((K, T)) * s)
    p_w = pack_weight(n((K, N)) / np.sqrt(K) / s, "e4m3")
    p_wx = pack_weight(n((L, N)) / np.sqrt(L) / s2, "e2m1")
    return {
        "tab_words": p_tab[0],
        "tab_scales": p_tab[1],
        "w_words": p_w[0],
        "w_scales": p_w[1],
        "x": (n((L, J)) * s2).astype(np.float32),
        "wx_words": p_wx[0],
        "wx_scales": p_wx[1],
        "iw0": (np.random.uniform(0.1, 0.6, J)).astype(np.float32),
        "iw1": (np.random.uniform(0.1, 0.6, J)).astype(np.float32),
        "offs": striped(np.concatenate([np.random.permutation(T)[:J] for _ in range(2)])),
    }


def reference(tab_words, tab_scales, w_words, w_scales, x, wx_words, wx_scales, iw0, iw1, offs):
    idx = unstriped(offs).reshape(2, J)
    tab_ = unpack_table4(tab_words, tab_scales)[:, idx]
    w_ = unpack_weight(w_words, w_scales, "e4m3")
    a0 = w_.T @ tab_[:, 0]
    a1 = w_.T @ tab_[:, 1]
    x_ = mxq(f64(x), 0, "e4m3")
    wx_ = unpack_weight(wx_words, wx_scales, "e2m1")
    ax = wx_.T @ x_
    return np.maximum(a0 * f64(iw0)[None, :] + a1 * f64(iw1)[None, :] + ax, 0.0)

@@ -1,0 +1,196 @@
+from contextlib import ExitStack
+
+import concourse.mybir as mybir
+from concourse.masks import make_identity
+
+K, L, N, T, J = 1024, 1024, 512, 2048, 512
+FLOPS = 2 * (2 * K + L) * N * J
+
+F32 = mybir.dt.float32
+BF16 = mybir.dt.bfloat16
+I32 = mybir.dt.int32
+U32 = mybir.dt.uint32
+U16 = mybir.dt.uint16
+U8 = mybir.dt.uint8
+FP8X4 = mybir.dt.float8_e4m3fn_x4
+FP4X4 = mybir.dt.float4_e2m1fn_x4
+MULT = mybir.AluOpType.mult
+ADD = mybir.AluOpType.add
+COPY = mybir.ActivationFunctionType.Copy
+RELU = mybir.ActivationFunctionType.Relu
+
+P = 128
+PACK = 4
+PASSES = 2
+LISTS = 2
+HALF = 256
+HALVES = J // HALF
+TILES = J // P
+
+
+def tile_list_interp_relu_kernel(
+    tc, tab_words, tab_scales, w_words, w_scales, x, wx_words, wx_scales, iw0, iw1, offs, out
+):
+    nc = tc.nc
+    with ExitStack() as ctx:
+        keep = ctx.enter_context(tc.tile_pool(name="keep", bufs=1))
+        psum = ctx.enter_context(tc.psum_pool(name="psum", bufs=2))
+
+        offsets = keep.tile([P, LISTS * J // 16], U16, name="offsets")
+        tab_z = keep.tile([P, T], U8, name="tab_z", align_bytes=64)
+        tab_w = keep.tile([P, T], I32, name="tab_w", align_bytes=64)
+        w_z = keep.tile([P, PASSES, N], U8, name="w_z", align_bytes=64)
+        wx_z = keep.tile([P, PASSES, N], U8, name="wx_z", align_bytes=64)
+        w_w = keep.tile([P, PASSES, N], I32, name="w_w", align_bytes=64)
+        wx_w = keep.tile([P, PASSES, 2 * N], U8, name="wx_w", align_bytes=64)
+        moved_z = [keep.tile([P, LISTS * HALF], U8, name="moved_z%d" % h, align_bytes=64) for h in range(HALVES)]
+        iw = [keep.tile([P, TILES], F32, name="iw%d" % g) for g in range(LISTS)]
+        ident = keep.tile([P, P], F32, name="ident")
+        warm = keep.tile([P, 1], F32, name="warm")
+
+        nc.gpsimd.memset(tab_z[:].bitcast(I32), 0)
+        nc.vector.memset(wx_z[:].rearrange("p a n -> p (a n)").bitcast(I32), 0)
+        nc.vector.memset(w_z[:].rearrange("p a n -> p (a n)").bitcast(I32), 0)
+        for h in range(HALVES):
+            nc.vector.memset(moved_z[h][:].bitcast(I32), 0)
+        nc.vector.memset(warm[:], 0.0)
+        nc.scalar.activation(out=warm[:], in_=warm[:], func=RELU)
+
+        def load_weight(g, src):
+            with nc.allow_non_contiguous_dma(reason="one weight a partition"):
+                nc.sync.dma_start(out=iw[g][:], in_=src.rearrange("(c p) -> p c", p=P))
+
+        nc.sync.dma_start(offsets[:], offs)
+        load_weight(0, iw0)
+        for q in range(4):
+            nc.sync.dma_start(
+                out=tab_z[32 * q : 32 * q + 8, :].bitcast(I32),
+                in_=tab_scales[:, 4 * q : 4 * q + 4, :].bitcast(I32),
+            )
+        nc.sync.dma_start(out=tab_w[:], in_=tab_words[0].rearrange("p t b -> p (t b)").bitcast(I32))
+
+        def load_scales(queue, plane, src):
+            for q in range(4):
+                queue.dma_start(
+                    out=plane[32 * q : 32 * q + 4, :, :].bitcast(I32),
+                    in_=src[:, 4 * q : 4 * q + 4, :].rearrange("a r n -> r a n").bitcast(I32),
+                )
+
+        x_raw = {}
+
+        def load_x(h, a):
+            x_raw[h, a] = keep.tile([P, PACK, HALF], F32, name="x_raw%d%d" % (h, a))
+            nc.sync.dma_start(
+                out=x_raw[h, a][:],
+                in_=x[512 * a : 512 * (a + 1), HALF * h : HALF * (h + 1)].rearrange("(p t) j -> p t j", t=PACK),
+            )
+
+        load_x(0, 0)
+        nc.sync.dma_start(out=w_w[:], in_=w_words.rearrange("a p n b -> p a (n b)").bitcast(I32))
+        load_scales(nc.sync, w_z, w_scales)
+        load_weight(1, iw1)
+        load_x(0, 1)
+        load_scales(nc.gpsimd, wx_z, wx_scales)
+        nc.sync.dma_start(out=wx_w[:].bitcast(I32), in_=wx_words.rearrange("a p n -> p a n").bitcast(I32))
+        load_x(1, 0)
+        load_x(1, 1)
+
+        make_identity(nc, ident[:])
+
+        planes = []
+        for h in range(HALVES):
+            picked_z = keep.tile([P, LISTS * HALF], U8, name="picked_z%d" % h, align_bytes=64)
+            for g in range(LISTS):
+                c0 = (g * J + h * HALF) // 16
+                nc.vector.tensor_copy(
+                    picked_z[:, g * HALF : (g + 1) * HALF], tab_z[:].indirect(offsets[:, c0 : c0 + HALF // 16])
+                )
+            nc.scalar.dma_start(out=moved_z[h][0:112, :].bitcast(I32), in_=picked_z[4:116, :].bitcast(I32))
+            planes.append((picked_z, moved_z[h]))
+
+        parted = {}
+        for h in range(HALVES):
+            picked_w = []
+            for g in range(LISTS):
+                c0 = (g * J + h * HALF) // 16
+                words = keep.tile([P, HALF], U32, name="picked_w%d" % g, align_bytes=64)
+                nc.vector.tensor_copy(words[:], tab_w[:].bitcast(U32).indirect(offsets[:, c0 : c0 + HALF // 16]))
+                picked_w.append(words)
+            for g in range(LISTS):
+                parted[h, g] = keep.tile([P, PASSES, HALF], U16, name="parted%d%d" % (h, g), align_bytes=64)
+                nc.vector.tensor_copy(
+                    parted[h, g][:], picked_w[g][:].bitcast(U16).rearrange("p (c a) -> p a c", a=PASSES)
+                )
+
+        x_codes, x_z = {}, {}
+        mixed = {}
+
+        def quantise(h, a):
+            grouped = keep.tile([P, HALF, PACK], BF16, name="grouped%d%d" % (h, a), align_bytes=64)
+            nc.scalar.copy(
+                out=grouped[:].rearrange("p (c i) t -> p c t i", i=4),
+                in_=x_raw[h, a][:].rearrange("p t (c i) -> p c t i", i=4),
+            )
+            x_codes[h, a] = keep.tile([P, HALF], U32, name="x_codes%d%d" % (h, a), align_bytes=64)
+            x_z[h, a] = keep.tile([P, HALF], U8, name="x_z%d%d" % (h, a), align_bytes=64)
+            nc.vector.quantize_mx(
+                out=x_codes[h, a][:].bitcast(FP8X4),
+                scales=x_z[h, a][:],
+                in_=grouped[:].rearrange("p j t -> p (j t)"),
+            )
+
+        def neighbours(jt):
+            h, s = divmod(jt, HALF // P)
+            acc = []
+            for g in range(LISTS):
+                bank = psum.tile([P, N], F32, name="acc%d" % g)
+                for a in range(PASSES):
+                    z0 = g * HALF + s * P
+                    nc.tensor.matmul_mx(
+                        out=bank[:],
+                        lhsT=parted[h, g][:, a, s * P : (s + 1) * P].bitcast(FP4X4),
+                        lhsT_scale=planes[h][a][:, z0 : z0 + P],
+                        rhs=w_w[:, a, :].bitcast(FP8X4),
+                        rhs_scale=w_z[:, a, :],
+                        start=(a == 0),
+                        stop=(a == PASSES - 1),
+                    )
+                acc.append(bank)
+            first = keep.tile([P, N], F32, name="first%d" % jt)
+            nc.scalar.activation(out=first[:], in_=acc[0][:], func=COPY, scale=iw[0][:, jt : jt + 1])
+            mixed[jt] = keep.tile([P, N], F32, name="mixed%d" % jt)
+            nc.vector.scalar_tensor_tensor(
+                out=mixed[jt][:], in0=acc[1][:], scalar=iw[1][:, jt : jt + 1], in1=first[:], op0=MULT, op1=ADD
+            )
+
+        def finish(jt):
+            h, s = divmod(jt, HALF // P)
+            bank = psum.tile([P, N], F32, name="accx")
+            for a in range(PASSES):
+                nc.tensor.matmul_mx(
+                    out=bank[:],
+                    lhsT=x_codes[h, a][:, s * P : (s + 1) * P].bitcast(FP8X4),
+                    lhsT_scale=x_z[h, a][:, s * P : (s + 1) * P],
+                    rhs=wx_w[:, a, :].bitcast(FP4X4),
+                    rhs_scale=wx_z[:, a, :],
+                    start=(a == 0),
+                    stop=(a == PASSES - 1),
+                )
+            total = keep.tile([P, N], F32, name="total%d" % jt)
+            nc.vector.tensor_tensor(out=total[:], in0=bank[:], in1=mixed[jt][:], op=ADD)
+            turned = psum.tile([P, N // P, P], F32, name="turned")
+            for nt in range(N // P):
+                nc.tensor.transpose(turned[:, nt, :], total[:, nt * P : (nt + 1) * P], ident[:])
+            result = keep.tile([P, N // P, P], F32, name="result%d" % jt)
+            nc.scalar.activation(out=result[:], in_=turned[:], func=RELU)
+            nc.sync.dma_start(
+                out=out[:, jt * P : (jt + 1) * P].rearrange("(nt p) j -> p nt j", p=P), in_=result[:]
+            )
+
+        for h in range(HALVES):
+            for s in range(HALF // P):
+                neighbours(2 * h + s)
+            for a in range(PASSES):
+                quantise(h, a)
+        for jt in range(TILES):
+            finish(jt)

@@ -21,11 +21,16 @@ RELU = mybir.ActivationFunctionType.Relu
 
 P = 128
 PACK = 4
-PASSES = 2
+K_PASS = P * PACK
+PASSES = K // K_PASS
 LISTS = 2
-HALF = 256
-HALVES = J // HALF
+QUADS = 4
+SCALE_ROWS = 4
+SECOND = 16
+LIST_ROWS = 16
 TILES = J // P
+HALF = J // 2
+BANKS = 8
 
 
 def tile_list_interp_relu_kernel(
@@ -34,163 +39,172 @@ def tile_list_interp_relu_kernel(
     nc = tc.nc
     with ExitStack() as ctx:
         keep = ctx.enter_context(tc.tile_pool(name="keep", bufs=1))
-        psum = ctx.enter_context(tc.psum_pool(name="psum", bufs=2))
+        psum = ctx.enter_context(tc.psum_pool(name="psum", bufs=BANKS))
 
-        offsets = keep.tile([P, LISTS * J // 16], U16, name="offsets")
-        tab_z = keep.tile([P, T], U8, name="tab_z", align_bytes=64)
-        tab_w = keep.tile([P, T], I32, name="tab_w", align_bytes=64)
-        w_z = keep.tile([P, PASSES, N], U8, name="w_z", align_bytes=64)
-        wx_z = keep.tile([P, PASSES, N], U8, name="wx_z", align_bytes=64)
-        w_w = keep.tile([P, PASSES, N], I32, name="w_w", align_bytes=64)
-        wx_w = keep.tile([P, PASSES, 2 * N], U8, name="wx_w", align_bytes=64)
-        moved_z = [keep.tile([P, LISTS * HALF], U8, name="moved_z%d" % h, align_bytes=64) for h in range(HALVES)]
-        iw = [keep.tile([P, TILES], F32, name="iw%d" % g) for g in range(LISTS)]
+        offsets = keep.tile([P, LISTS * J // LIST_ROWS], U16, name="offsets")
+        tab_plane = keep.tile([P, T], U8, name="tab_plane", align_bytes=64)
+        tab_codes = keep.tile([P, T], I32, name="tab_codes", align_bytes=64)
+        w_planes = keep.tile([P, PASSES, N], U8, name="w_planes", align_bytes=64)
+        w_codes = keep.tile([P, PASSES, N], I32, name="w_codes", align_bytes=64)
+        wx_planes = keep.tile([P, PASSES, N], U8, name="wx_planes", align_bytes=64)
+        wx_codes = keep.tile([P, PASSES, 2 * N], U8, name="wx_codes", align_bytes=64)
+        iw_rows = keep.tile([P, P], F32, name="iw_rows", tag="early", align_bytes=64)
+        iw = keep.tile([P, LISTS, TILES], F32, name="iw")
         ident = keep.tile([P, P], F32, name="ident")
-        warm = keep.tile([P, 1], F32, name="warm")
 
-        nc.gpsimd.memset(tab_z[:].bitcast(I32), 0)
-        nc.vector.memset(wx_z[:].rearrange("p a n -> p (a n)").bitcast(I32), 0)
-        nc.vector.memset(w_z[:].rearrange("p a n -> p (a n)").bitcast(I32), 0)
-        for h in range(HALVES):
-            nc.vector.memset(moved_z[h][:].bitcast(I32), 0)
-        nc.vector.memset(warm[:], 0.0)
-        nc.scalar.activation(out=warm[:], in_=warm[:], func=RELU)
-
-        def load_weight(g, src):
-            with nc.allow_non_contiguous_dma(reason="one weight a partition"):
-                nc.sync.dma_start(out=iw[g][:], in_=src.rearrange("(c p) -> p c", p=P))
-
-        nc.sync.dma_start(offsets[:], offs)
-        load_weight(0, iw0)
-        for q in range(4):
-            nc.sync.dma_start(
-                out=tab_z[32 * q : 32 * q + 8, :].bitcast(I32),
-                in_=tab_scales[:, 4 * q : 4 * q + 4, :].bitcast(I32),
-            )
-        nc.sync.dma_start(out=tab_w[:], in_=tab_words[0].rearrange("p t b -> p (t b)").bitcast(I32))
-
-        def load_scales(queue, plane, src):
-            for q in range(4):
-                queue.dma_start(
-                    out=plane[32 * q : 32 * q + 4, :, :].bitcast(I32),
-                    in_=src[:, 4 * q : 4 * q + 4, :].rearrange("a r n -> r a n").bitcast(I32),
-                )
-
-        x_raw = {}
-
-        def load_x(h, a):
-            x_raw[h, a] = keep.tile([P, PACK, HALF], F32, name="x_raw%d%d" % (h, a))
-            nc.sync.dma_start(
-                out=x_raw[h, a][:],
-                in_=x[512 * a : 512 * (a + 1), HALF * h : HALF * (h + 1)].rearrange("(p t) j -> p t j", t=PACK),
-            )
-
-        load_x(0, 0)
-        nc.sync.dma_start(out=w_w[:], in_=w_words.rearrange("a p n b -> p a (n b)").bitcast(I32))
-        load_scales(nc.sync, w_z, w_scales)
-        load_weight(1, iw1)
-        load_x(0, 1)
-        load_scales(nc.gpsimd, wx_z, wx_scales)
-        nc.sync.dma_start(out=wx_w[:].bitcast(I32), in_=wx_words.rearrange("a p n -> p a n").bitcast(I32))
-        load_x(1, 0)
-        load_x(1, 1)
-
+        nc.vector.memset(iw_rows[:], 0.0)
+        nc.gpsimd.memset(tab_plane[:].bitcast(I32), 0)
+        for planes in (wx_planes, w_planes):
+            nc.vector.memset(planes[:].rearrange("p a n -> p (a n)").bitcast(I32), 0)
         make_identity(nc, ident[:])
 
-        planes = []
-        for h in range(HALVES):
-            picked_z = keep.tile([P, LISTS * HALF], U8, name="picked_z%d" % h, align_bytes=64)
-            for g in range(LISTS):
-                c0 = (g * J + h * HALF) // 16
-                nc.vector.tensor_copy(
-                    picked_z[:, g * HALF : (g + 1) * HALF], tab_z[:].indirect(offsets[:, c0 : c0 + HALF // 16])
-                )
-            nc.scalar.dma_start(out=moved_z[h][0:112, :].bitcast(I32), in_=picked_z[4:116, :].bitcast(I32))
-            planes.append((picked_z, moved_z[h]))
-
-        parted = {}
-        for h in range(HALVES):
-            picked_w = []
-            for g in range(LISTS):
-                c0 = (g * J + h * HALF) // 16
-                words = keep.tile([P, HALF], U32, name="picked_w%d" % g, align_bytes=64)
-                nc.vector.tensor_copy(words[:], tab_w[:].bitcast(U32).indirect(offsets[:, c0 : c0 + HALF // 16]))
-                picked_w.append(words)
-            for g in range(LISTS):
-                parted[h, g] = keep.tile([P, PASSES, HALF], U16, name="parted%d%d" % (h, g), align_bytes=64)
-                nc.vector.tensor_copy(
-                    parted[h, g][:], picked_w[g][:].bitcast(U16).rearrange("p (c a) -> p a c", a=PASSES)
+        def load_planes(queue, planes, scales):
+            for quad in range(QUADS):
+                queue.dma_start(
+                    out=planes[32 * quad : 32 * quad + SCALE_ROWS, :, :].bitcast(I32),
+                    in_=scales[:, SCALE_ROWS * quad : SCALE_ROWS * (quad + 1), :].rearrange("a r n -> r a n").bitcast(I32),
                 )
 
-        x_codes, x_z = {}, {}
-        mixed = {}
+        def load_x(half, a):
+            name = "x_raw%d%d" % (half, a)
+            raw = keep.tile([P, PACK, HALF], F32, name=name, tag=name)
+            rows = x[K_PASS * a : K_PASS * (a + 1), HALF * half : HALF * (half + 1)]
+            nc.sync.dma_start(out=raw[:], in_=rows.rearrange("(p t) j -> p t j", t=PACK))
+            return raw
 
-        def quantise(h, a):
-            grouped = keep.tile([P, HALF, PACK], BF16, name="grouped%d%d" % (h, a), align_bytes=64)
-            nc.scalar.copy(
-                out=grouped[:].rearrange("p (c i) t -> p c t i", i=4),
-                in_=x_raw[h, a][:].rearrange("p t (c i) -> p c t i", i=4),
+        nc.sync.dma_start(offsets[:], offs)
+        for g, weights in enumerate((iw0, iw1)):
+            nc.sync.dma_start(out=iw_rows[32 * g : 32 * g + TILES, :], in_=weights.rearrange("(c p) -> c p", p=P))
+        for r in range(SCALE_ROWS):
+            nc.sync.dma_start(
+                out=tab_plane[r:P:SECOND, :].bitcast(I32),
+                in_=tab_scales[:, r : QUADS * SCALE_ROWS : SCALE_ROWS, :].rearrange("a q t -> q a t").bitcast(I32),
             )
-            x_codes[h, a] = keep.tile([P, HALF], U32, name="x_codes%d%d" % (h, a), align_bytes=64)
-            x_z[h, a] = keep.tile([P, HALF], U8, name="x_z%d%d" % (h, a), align_bytes=64)
+        nc.sync.dma_start(out=tab_codes[:], in_=tab_words[0].rearrange("p t b -> p (t b)").bitcast(I32))
+        nc.sync.dma_start(out=w_codes[:], in_=w_words.rearrange("a p n b -> p a (n b)").bitcast(I32))
+        load_planes(nc.sync, w_planes, w_scales)
+        x_raw = {key: load_x(*key) for key in ((0, 0), (0, 1), (1, 0))}
+        nc.sync.dma_start(out=wx_codes[:].bitcast(I32), in_=wx_words.rearrange("a p n -> p a n").bitcast(I32))
+        x_raw[1, 1] = load_x(1, 1)
+        load_planes(nc.gpsimd, wx_planes, wx_scales)
+
+        iw_turned = psum.tile([P, LISTS * 2, 32], F32, name="iw_turned", tag="bank")
+        nc.tensor.transpose(iw_turned[:].rearrange("p g c -> p (g c)"), iw_rows[:], ident[:])
+        nc.scalar.copy(out=iw[:], in_=iw_turned[:, 0:LISTS, 0:TILES])
+
+        picked_plane = keep.tile([P, LISTS * J], U8, name="picked_plane", align_bytes=64)
+        nc.vector.tensor_copy(picked_plane[:], tab_plane[:].indirect(offsets[:]))
+        moved_plane = keep.tile([P, LISTS * J], U8, name="moved_plane", tag="early", align_bytes=64)
+        nc.vector.memset(moved_plane[:].bitcast(I32), 0)
+        nc.scalar.dma_start(out=moved_plane[0 : P - SECOND, :].bitcast(I32), in_=picked_plane[SECOND:P, :].bitcast(I32))
+        v_planes = (picked_plane, moved_plane)
+
+        def gather_words(first, count, tag):
+            words = keep.tile([P, count], U32, name="picked%d" % first, tag=tag, align_bytes=64)
+            columns = slice(first // LIST_ROWS, (first + count) // LIST_ROWS)
+            nc.vector.tensor_copy(words[:], tab_codes[:].bitcast(U32).indirect(offsets[:, columns]))
+            return words
+
+        v_codes = {}
+
+        def part_words(first, count, words):
+            parted = keep.tile([P, PASSES, count], U16, name="parted%d" % first, align_bytes=64)
+            nc.vector.tensor_copy(parted[:], words[:].bitcast(U16).rearrange("p (c a) -> p a c", a=PASSES))
+            for c in range(0, count, P):
+                g, jt = divmod((first + c) // P, TILES)
+                v_codes[g, jt] = parted[:, :, c : c + P]
+
+        halves = [gather_words(HALF * half, HALF, "picked%d" % half) for half in range(2)]
+        for half in range(2):
+            part_words(HALF * half, HALF, halves[half])
+        part_words(J, J, gather_words(J, J, "picked0"))
+
+        acc = {}
+
+        def table_pass(g, jt, a):
+            if a == 0:
+                acc[g, jt] = psum.tile([P, N], F32, name="acc%d%d" % (g, jt), tag="bank")
+            entry = g * J + jt * P
+            nc.tensor.matmul_mx(
+                out=acc[g, jt][:],
+                lhsT=v_codes[g, jt][:, a, :].bitcast(FP4X4),
+                lhsT_scale=v_planes[a][:, entry : entry + P],
+                rhs=w_codes[:, a, :].bitcast(FP8X4),
+                rhs_scale=w_planes[:, a, :],
+                start=(a == 0),
+                stop=(a == PASSES - 1),
+            )
+
+        for a in range(PASSES):
+            for g in range(LISTS):
+                for jt in range(TILES):
+                    table_pass(g, jt, a)
+
+        grouped, x_codes, x_planes = {}, {}, {}
+
+        def interleave(half, a, copy):
+            name = "grouped%d%d" % (half, a)
+            grouped[half, a] = keep.tile([P, HALF, PACK], BF16, name=name, tag=name, align_bytes=64)
+            copy(
+                out=grouped[half, a][:].rearrange("p (c i) t -> p c t i", i=4),
+                in_=x_raw[half, a][:].rearrange("p t (c i) -> p c t i", i=4),
+            )
+
+        def quantise(half, a):
+            x_codes[half, a] = keep.tile([P, HALF], U32, name="x_codes%d%d" % (half, a), align_bytes=64)
+            x_planes[half, a] = keep.tile([P, HALF], U8, name="x_plane%d%d" % (half, a), align_bytes=64)
             nc.vector.quantize_mx(
-                out=x_codes[h, a][:].bitcast(FP8X4),
-                scales=x_z[h, a][:],
-                in_=grouped[:].rearrange("p j t -> p (j t)"),
+                out=x_codes[half, a][:].bitcast(FP8X4),
+                scales=x_planes[half, a][:],
+                in_=grouped[half, a][:].rearrange("p j t -> p (j t)"),
             )
 
-        def neighbours(jt):
-            h, s = divmod(jt, HALF // P)
-            acc = []
-            for g in range(LISTS):
-                bank = psum.tile([P, N], F32, name="acc%d" % g)
-                for a in range(PASSES):
-                    z0 = g * HALF + s * P
-                    nc.tensor.matmul_mx(
-                        out=bank[:],
-                        lhsT=parted[h, g][:, a, s * P : (s + 1) * P].bitcast(FP4X4),
-                        lhsT_scale=planes[h][a][:, z0 : z0 + P],
-                        rhs=w_w[:, a, :].bitcast(FP8X4),
-                        rhs_scale=w_z[:, a, :],
-                        start=(a == 0),
-                        stop=(a == PASSES - 1),
-                    )
-                acc.append(bank)
-            first = keep.tile([P, N], F32, name="first%d" % jt)
-            nc.scalar.activation(out=first[:], in_=acc[0][:], func=COPY, scale=iw[0][:, jt : jt + 1])
-            mixed[jt] = keep.tile([P, N], F32, name="mixed%d" % jt)
+        interleave(0, 0, nc.scalar.copy)
+        interleave(0, 1, nc.scalar.copy)
+        quantise(0, 0)
+        interleave(1, 0, nc.vector.tensor_copy)
+        quantise(0, 1)
+        quantise(1, 0)
+
+        first = keep.tile([P, TILES, N], F32, name="first", tag="x_raw01")
+        mixed = keep.tile([P, TILES, N], F32, name="mixed")
+        for jt in range(TILES):
+            nc.scalar.activation(out=first[:, jt, :], in_=acc[0, jt][:], func=COPY, scale=iw[:, 0, jt : jt + 1])
+        for jt in range(TILES):
             nc.vector.scalar_tensor_tensor(
-                out=mixed[jt][:], in0=acc[1][:], scalar=iw[1][:, jt : jt + 1], in1=first[:], op0=MULT, op1=ADD
+                out=mixed[:, jt, :], in0=acc[1, jt][:], scalar=iw[:, 1, jt : jt + 1], in1=first[:, jt, :], op0=MULT, op1=ADD
+            )
+        interleave(1, 1, nc.scalar.copy)
+        quantise(1, 1)
+
+        skip = {}
+
+        def skip_pass(jt, a):
+            if a == 0:
+                skip[jt] = psum.tile([P, N], F32, name="skip%d" % jt, tag="bank")
+            half, c = divmod(jt * P, HALF)
+            nc.tensor.matmul_mx(
+                out=skip[jt][:],
+                lhsT=x_codes[half, a][:, c : c + P].bitcast(FP8X4),
+                lhsT_scale=x_planes[half, a][:, c : c + P],
+                rhs=wx_codes[:, a, :].bitcast(FP4X4),
+                rhs_scale=wx_planes[:, a, :],
+                start=(a == 0),
+                stop=(a == PASSES - 1),
             )
 
-        def finish(jt):
-            h, s = divmod(jt, HALF // P)
-            bank = psum.tile([P, N], F32, name="accx")
+        for half in range(2):
             for a in range(PASSES):
-                nc.tensor.matmul_mx(
-                    out=bank[:],
-                    lhsT=x_codes[h, a][:, s * P : (s + 1) * P].bitcast(FP8X4),
-                    lhsT_scale=x_z[h, a][:, s * P : (s + 1) * P],
-                    rhs=wx_w[:, a, :].bitcast(FP4X4),
-                    rhs_scale=wx_z[:, a, :],
-                    start=(a == 0),
-                    stop=(a == PASSES - 1),
-                )
-            total = keep.tile([P, N], F32, name="total%d" % jt)
-            nc.vector.tensor_tensor(out=total[:], in0=bank[:], in1=mixed[jt][:], op=ADD)
-            turned = psum.tile([P, N // P, P], F32, name="turned")
+                for jt in (2 * half, 2 * half + 1):
+                    skip_pass(jt, a)
+
+        total = keep.tile([P, TILES, N], F32, name="total", tag="grouped11", align_bytes=64)
+        for jt in range(TILES):
+            nc.vector.tensor_tensor(out=total[:, jt, :], in0=skip[jt][:], in1=mixed[:, jt, :], op=ADD)
+        for jt in range(TILES):
+            turned = psum.tile([P, N // P, P], F32, name="turned%d" % jt, tag="bank")
             for nt in range(N // P):
-                nc.tensor.transpose(turned[:, nt, :], total[:, nt * P : (nt + 1) * P], ident[:])
+                nc.tensor.transpose(turned[:, nt, :], total[:, jt, nt * P : (nt + 1) * P], ident[:])
             result = keep.tile([P, N // P, P], F32, name="result%d" % jt)
             nc.scalar.activation(out=result[:], in_=turned[:], func=RELU)
-            nc.sync.dma_start(
-                out=out[:, jt * P : (jt + 1) * P].rearrange("(nt p) j -> p nt j", p=P), in_=result[:]
-            )
-
-        for h in range(HALVES):
-            for s in range(HALF // P):
-                neighbours(2 * h + s)
-            for a in range(PASSES):
-                quantise(h, a)
-        for jt in range(TILES):
-            finish(jt)
+            nc.sync.dma_start(out=out[:, jt * P : (jt + 1) * P].rearrange("(nt p) j -> p nt j", p=P), in_=result[:])

@@ -48,15 +48,17 @@ def tile_list_interp_relu_kernel(
         w_codes = keep.tile([P, PASSES, N], I32, name="w_codes", align_bytes=64)
         wx_planes = keep.tile([P, PASSES, N], U8, name="wx_planes", align_bytes=64)
         wx_codes = keep.tile([P, PASSES, 2 * N], U8, name="wx_codes", align_bytes=64)
-        iw_rows = keep.tile([P, P], F32, name="iw_rows", tag="early", align_bytes=64)
-        iw = keep.tile([P, LISTS, TILES], F32, name="iw")
+        picked_plane = keep.tile([P, LISTS * J], U8, name="picked_plane", align_bytes=64)
+        moved_plane = keep.tile([P, LISTS * J], U8, name="moved_plane", align_bytes=64)
+        iw_rows = keep.tile([P, TILES, 32], F32, name="iw_rows", align_bytes=64)
+        iw = keep.tile([P, TILES, 32], F32, name="iw", align_bytes=64)
         ident = keep.tile([P, P], F32, name="ident")
 
         nc.vector.memset(iw_rows[:], 0.0)
         nc.gpsimd.memset(tab_plane[:].bitcast(I32), 0)
         for planes in (wx_planes, w_planes):
             nc.vector.memset(planes[:].rearrange("p a n -> p (a n)").bitcast(I32), 0)
-        make_identity(nc, ident[:])
+        nc.vector.memset(moved_plane[:].bitcast(I32), 0)
 
         def load_planes(queue, planes, scales):
             for quad in range(QUADS):
@@ -65,16 +67,20 @@ def tile_list_interp_relu_kernel(
                     in_=scales[:, SCALE_ROWS * quad : SCALE_ROWS * (quad + 1), :].rearrange("a r n -> r a n").bitcast(I32),
                 )
 
-        def load_x(half, a):
-            name = "x_raw%d%d" % (half, a)
-            raw = keep.tile([P, PACK, HALF], F32, name=name, tag=name)
-            rows = x[K_PASS * a : K_PASS * (a + 1), HALF * half : HALF * (half + 1)]
+        x_raw = {}
+
+        def load_x(a, halves):
+            name = "x_raw%d%d" % (halves[0], a)
+            width = HALF * len(halves)
+            raw = keep.tile([P, PACK, width], F32, name=name, tag=name)
+            rows = x[K_PASS * a : K_PASS * (a + 1), HALF * halves[0] : HALF * halves[0] + width]
             nc.sync.dma_start(out=raw[:], in_=rows.rearrange("(p t) j -> p t j", t=PACK))
-            return raw
+            for i, half in enumerate(halves):
+                x_raw[half, a] = raw[:, :, HALF * i : HALF * (i + 1)]
 
         nc.sync.dma_start(offsets[:], offs)
         for g, weights in enumerate((iw0, iw1)):
-            nc.sync.dma_start(out=iw_rows[32 * g : 32 * g + TILES, :], in_=weights.rearrange("(c p) -> c p", p=P))
+            nc.sync.dma_start(out=iw_rows[g:P:32, :, :], in_=weights.rearrange("(c q i) -> q c i", q=QUADS, i=32))
         for r in range(SCALE_ROWS):
             nc.sync.dma_start(
                 out=tab_plane[r:P:SECOND, :].bitcast(I32),
@@ -83,19 +89,16 @@ def tile_list_interp_relu_kernel(
         nc.sync.dma_start(out=tab_codes[:], in_=tab_words[0].rearrange("p t b -> p (t b)").bitcast(I32))
         nc.sync.dma_start(out=w_codes[:], in_=w_words.rearrange("a p n b -> p a (n b)").bitcast(I32))
         load_planes(nc.sync, w_planes, w_scales)
-        x_raw = {key: load_x(*key) for key in ((0, 0), (0, 1), (1, 0))}
+        load_x(0, (0,))
+        load_x(0, (1,))
+        load_x(1, (0, 1))
         nc.sync.dma_start(out=wx_codes[:].bitcast(I32), in_=wx_words.rearrange("a p n -> p a n").bitcast(I32))
-        x_raw[1, 1] = load_x(1, 1)
         load_planes(nc.gpsimd, wx_planes, wx_scales)
+        make_identity(nc, ident[:])
 
-        iw_turned = psum.tile([P, LISTS * 2, 32], F32, name="iw_turned", tag="bank")
-        nc.tensor.transpose(iw_turned[:].rearrange("p g c -> p (g c)"), iw_rows[:], ident[:])
-        nc.scalar.copy(out=iw[:], in_=iw_turned[:, 0:LISTS, 0:TILES])
+        nc.vector.transpose(iw[:].rearrange("p c i -> p (c i)"), iw_rows[:].rearrange("p c i -> p (c i)"))
 
-        picked_plane = keep.tile([P, LISTS * J], U8, name="picked_plane", align_bytes=64)
         nc.vector.tensor_copy(picked_plane[:], tab_plane[:].indirect(offsets[:]))
-        moved_plane = keep.tile([P, LISTS * J], U8, name="moved_plane", tag="early", align_bytes=64)
-        nc.vector.memset(moved_plane[:].bitcast(I32), 0)
         nc.scalar.dma_start(out=moved_plane[0 : P - SECOND, :].bitcast(I32), in_=picked_plane[SECOND:P, :].bitcast(I32))
         v_planes = (picked_plane, moved_plane)
 
@@ -147,7 +150,7 @@ def tile_list_interp_relu_kernel(
             grouped[half, a] = keep.tile([P, HALF, PACK], BF16, name=name, tag=name, align_bytes=64)
             copy(
                 out=grouped[half, a][:].rearrange("p (c i) t -> p c t i", i=4),
-                in_=x_raw[half, a][:].rearrange("p t (c i) -> p c t i", i=4),
+                in_=x_raw[half, a].rearrange("p t (c i) -> p c t i", i=4),
             )
 
         def quantise(half, a):
@@ -159,20 +162,19 @@ def tile_list_interp_relu_kernel(
                 in_=grouped[half, a][:].rearrange("p j t -> p (j t)"),
             )
 
-        interleave(0, 0, nc.scalar.copy)
-        interleave(0, 1, nc.scalar.copy)
-        quantise(0, 0)
-        interleave(1, 0, nc.vector.tensor_copy)
+        for half in range(2):
+            interleave(half, 0, nc.scalar.copy)
+            quantise(half, 0)
+        interleave(0, 1, nc.vector.tensor_copy)
         quantise(0, 1)
-        quantise(1, 0)
 
-        first = keep.tile([P, TILES, N], F32, name="first", tag="x_raw01")
+        first = keep.tile([P, TILES, N], F32, name="first", tag="x_raw10")
         mixed = keep.tile([P, TILES, N], F32, name="mixed")
         for jt in range(TILES):
-            nc.scalar.activation(out=first[:, jt, :], in_=acc[0, jt][:], func=COPY, scale=iw[:, 0, jt : jt + 1])
+            nc.scalar.activation(out=first[:, jt, :], in_=acc[0, jt][:], func=COPY, scale=iw[:, jt, 0:1])
         for jt in range(TILES):
             nc.vector.scalar_tensor_tensor(
-                out=mixed[:, jt, :], in0=acc[1, jt][:], scalar=iw[:, 1, jt : jt + 1], in1=first[:, jt, :], op0=MULT, op1=ADD
+                out=mixed[:, jt, :], in0=acc[1, jt][:], scalar=iw[:, jt, 1:2], in1=first[:, jt, :], op0=MULT, op1=ADD
             )
         interleave(1, 1, nc.scalar.copy)
         quantise(1, 1)
@@ -201,10 +203,18 @@ def tile_list_interp_relu_kernel(
         total = keep.tile([P, TILES, N], F32, name="total", tag="grouped11", align_bytes=64)
         for jt in range(TILES):
             nc.vector.tensor_tensor(out=total[:, jt, :], in0=skip[jt][:], in1=mixed[:, jt, :], op=ADD)
-        for jt in range(TILES):
-            turned = psum.tile([P, N // P, P], F32, name="turned%d" % jt, tag="bank")
-            for nt in range(N // P):
-                nc.tensor.transpose(turned[:, nt, :], total[:, jt, nt * P : (nt + 1) * P], ident[:])
-            result = keep.tile([P, N // P, P], F32, name="result%d" % jt)
-            nc.scalar.activation(out=result[:], in_=turned[:], func=RELU)
-            nc.sync.dma_start(out=out[:, jt * P : (jt + 1) * P].rearrange("(nt p) j -> p nt j", p=P), in_=result[:])
+        for half in range(2):
+            turned = [psum.tile([P, 2, HALF], F32, name="turned%d%d" % (half, b), tag="bank") for b in range(2)]
+            for s in range(2):
+                for nt in range(N // P):
+                    nc.tensor.transpose(
+                        turned[nt // 2][:, nt % 2, s * P : (s + 1) * P], total[:, 2 * half + s, nt * P : (nt + 1) * P], ident[:]
+                    )
+            for b in range(2):
+                result = keep.tile([P, 2, HALF], F32, name="result%d%d" % (half, b))
+                if (half, b) == (1, 1):
+                    nc.vector.tensor_scalar_max(result[:], turned[b][:], 0.0)
+                else:
+                    nc.scalar.activation(out=result[:], in_=turned[b][:], func=RELU)
+                rows = out[2 * P * b : 2 * P * (b + 1), HALF * half : HALF * (half + 1)]
+                nc.sync.dma_start(out=rows.rearrange("(r p) j -> p r j", p=P), in_=result[:])

@@ -30,7 +30,6 @@ SECOND = 16
 LIST_ROWS = 16
 TILES = J // P
 HALF = J // 2
-BANKS = 8
 
 
 def tile_list_interp_relu_kernel(
@@ -39,26 +38,25 @@ def tile_list_interp_relu_kernel(
     nc = tc.nc
     with ExitStack() as ctx:
         keep = ctx.enter_context(tc.tile_pool(name="keep", bufs=1))
-        psum = ctx.enter_context(tc.psum_pool(name="psum", bufs=BANKS))
+        psum = ctx.enter_context(tc.psum_pool(name="psum", bufs=1))
 
         offsets = keep.tile([P, LISTS * J // LIST_ROWS], U16, name="offsets")
-        tab_plane = keep.tile([P, T], U8, name="tab_plane", align_bytes=64)
+        tab_plane = keep.tile([P, T], U8, name="tab_plane", tag="tab_plane", align_bytes=64)
         tab_codes = keep.tile([P, T], I32, name="tab_codes", align_bytes=64)
         w_planes = keep.tile([P, PASSES, N], U8, name="w_planes", align_bytes=64)
         w_codes = keep.tile([P, PASSES, N], I32, name="w_codes", align_bytes=64)
         wx_planes = keep.tile([P, PASSES, N], U8, name="wx_planes", align_bytes=64)
         wx_codes = keep.tile([P, PASSES, 2 * N], U8, name="wx_codes", align_bytes=64)
-        picked_plane = keep.tile([P, LISTS * J], U8, name="picked_plane", align_bytes=64)
-        moved_plane = keep.tile([P, LISTS * J], U8, name="moved_plane", align_bytes=64)
-        iw_rows = keep.tile([P, TILES, 32], F32, name="iw_rows", align_bytes=64)
-        iw = keep.tile([P, TILES, 32], F32, name="iw", align_bytes=64)
+        moved_planes = [keep.tile([P, J], U8, name="moved_plane%d" % g, align_bytes=64) for g in range(LISTS)]
+        iw = [keep.tile([P, TILES], F32, name="iw%d" % g) for g in range(LISTS)]
         ident = keep.tile([P, P], F32, name="ident")
 
-        nc.vector.memset(iw_rows[:], 0.0)
-        nc.gpsimd.memset(tab_plane[:].bitcast(I32), 0)
-        for planes in (wx_planes, w_planes):
+        nc.vector.memset(tab_plane[:, 0 : T // 2].bitcast(I32), 0)
+        nc.gpsimd.memset(tab_plane[:, T // 2 : T].bitcast(I32), 0)
+        for planes in (w_planes, wx_planes):
             nc.vector.memset(planes[:].rearrange("p a n -> p (a n)").bitcast(I32), 0)
-        nc.vector.memset(moved_plane[:].bitcast(I32), 0)
+        for plane in moved_planes:
+            nc.vector.memset(plane[P - 32 : P, :].bitcast(I32), 0)
 
         def load_planes(queue, planes, scales):
             for quad in range(QUADS):
@@ -70,37 +68,40 @@ def tile_list_interp_relu_kernel(
         x_raw = {}
 
         def load_x(a, halves):
-            name = "x_raw%d%d" % (halves[0], a)
             width = HALF * len(halves)
-            raw = keep.tile([P, PACK, width], F32, name=name, tag=name)
+            raw = keep.tile([P, PACK, width], F32, name="x_raw%d%d" % (halves[0], a))
             rows = x[K_PASS * a : K_PASS * (a + 1), HALF * halves[0] : HALF * halves[0] + width]
             nc.sync.dma_start(out=raw[:], in_=rows.rearrange("(p t) j -> p t j", t=PACK))
             for i, half in enumerate(halves):
                 x_raw[half, a] = raw[:, :, HALF * i : HALF * (i + 1)]
 
         nc.sync.dma_start(offsets[:], offs)
-        for g, weights in enumerate((iw0, iw1)):
-            nc.sync.dma_start(out=iw_rows[g:P:32, :, :], in_=weights.rearrange("(c q i) -> q c i", q=QUADS, i=32))
+        tab_rows = tab_words[0].rearrange("p t b -> p (t b)").bitcast(I32)
+        nc.sync.dma_start(out=tab_codes[:, 0 : T // 2], in_=tab_rows[:, 0 : T // 2])
         for r in range(SCALE_ROWS):
             nc.sync.dma_start(
                 out=tab_plane[r:P:SECOND, :].bitcast(I32),
                 in_=tab_scales[:, r : QUADS * SCALE_ROWS : SCALE_ROWS, :].rearrange("a q t -> q a t").bitcast(I32),
             )
-        nc.sync.dma_start(out=tab_codes[:], in_=tab_words[0].rearrange("p t b -> p (t b)").bitcast(I32))
+        nc.sync.dma_start(out=tab_codes[:, T // 2 : T], in_=tab_rows[:, T // 2 : T])
         nc.sync.dma_start(out=w_codes[:], in_=w_words.rearrange("a p n b -> p a (n b)").bitcast(I32))
         load_planes(nc.sync, w_planes, w_scales)
-        load_x(0, (0,))
-        load_x(0, (1,))
-        load_x(1, (0, 1))
-        nc.sync.dma_start(out=wx_codes[:].bitcast(I32), in_=wx_words.rearrange("a p n -> p a n").bitcast(I32))
+        load_x(0, (0, 1))
+        with nc.allow_non_contiguous_dma(reason="one weight a partition"):
+            for g, weights in enumerate((iw0, iw1)):
+                nc.gpsimd.dma_start(out=iw[g][:], in_=weights.rearrange("(c p) -> p c", p=P))
         load_planes(nc.gpsimd, wx_planes, wx_scales)
         make_identity(nc, ident[:])
 
-        nc.vector.transpose(iw[:].rearrange("p c i -> p (c i)"), iw_rows[:].rearrange("p c i -> p (c i)"))
+        v_planes, v_codes = {}, {}
 
-        nc.vector.tensor_copy(picked_plane[:], tab_plane[:].indirect(offsets[:]))
-        nc.scalar.dma_start(out=moved_plane[0 : P - SECOND, :].bitcast(I32), in_=picked_plane[SECOND:P, :].bitcast(I32))
-        v_planes = (picked_plane, moved_plane)
+        def gather_scales(g, tag):
+            picked = keep.tile([P, J], U8, name="picked_plane%d" % g, tag=tag, align_bytes=64)
+            columns = slice(g * J // LIST_ROWS, (g + 1) * J // LIST_ROWS)
+            nc.vector.tensor_copy(picked[:], tab_plane[:].indirect(offsets[:, columns]))
+            nc.sync.dma_start(out=moved_planes[g][0 : P - SECOND, :].bitcast(I32), in_=picked[SECOND:P, :].bitcast(I32))
+            for jt in range(TILES):
+                v_planes[g, jt] = (picked[:, jt * P : (jt + 1) * P], moved_planes[g][:, jt * P : (jt + 1) * P])
 
         def gather_words(first, count, tag):
             words = keep.tile([P, count], U32, name="picked%d" % first, tag=tag, align_bytes=64)
@@ -108,30 +109,31 @@ def tile_list_interp_relu_kernel(
             nc.vector.tensor_copy(words[:], tab_codes[:].bitcast(U32).indirect(offsets[:, columns]))
             return words
 
-        v_codes = {}
-
-        def part_words(first, count, words):
-            parted = keep.tile([P, PASSES, count], U16, name="parted%d" % first, align_bytes=64)
+        def part_words(first, count, words, tag):
+            parted = keep.tile([P, PASSES, count], U16, name="parted%d" % first, tag=tag, align_bytes=64)
             nc.vector.tensor_copy(parted[:], words[:].bitcast(U16).rearrange("p (c a) -> p a c", a=PASSES))
             for c in range(0, count, P):
-                g, jt = divmod((first + c) // P, TILES)
-                v_codes[g, jt] = parted[:, :, c : c + P]
+                v_codes[divmod((first + c) // P, TILES)] = parted[:, :, c : c + P]
 
-        halves = [gather_words(HALF * half, HALF, "picked%d" % half) for half in range(2)]
-        for half in range(2):
-            part_words(HALF * half, HALF, halves[half])
-        part_words(J, J, gather_words(J, J, "picked0"))
+        gather_scales(0, "picked_plane")
+        load_x(1, (0,))
+        words = [gather_words(HALF * half, HALF, "picked%d" % half) for half in range(2)]
+        part_words(0, HALF, words[0], "parted0")
+        gather_scales(1, "picked0")
+        nc.sync.dma_start(out=wx_codes[:].bitcast(I32), in_=wx_words.rearrange("a p n -> p a n").bitcast(I32))
+        load_x(1, (1,))
+        part_words(HALF, HALF, words[1], "tab_plane")
+        part_words(J, J, gather_words(J, J, "picked1"), "parted2")
 
         acc = {}
 
         def table_pass(g, jt, a):
             if a == 0:
-                acc[g, jt] = psum.tile([P, N], F32, name="acc%d%d" % (g, jt), tag="bank")
-            entry = g * J + jt * P
+                acc[g, jt] = psum.tile([P, N], F32, name="acc%d%d" % (g, jt), tag="bank%d" % jt)
             nc.tensor.matmul_mx(
                 out=acc[g, jt][:],
                 lhsT=v_codes[g, jt][:, a, :].bitcast(FP4X4),
-                lhsT_scale=v_planes[a][:, entry : entry + P],
+                lhsT_scale=v_planes[g, jt][a],
                 rhs=w_codes[:, a, :].bitcast(FP8X4),
                 rhs_scale=w_planes[:, a, :],
                 start=(a == 0),
@@ -139,11 +141,13 @@ def tile_list_interp_relu_kernel(
             )
 
         for a in range(PASSES):
-            for g in range(LISTS):
-                for jt in range(TILES):
-                    table_pass(g, jt, a)
+            for jt in range(TILES):
+                table_pass(0, jt, a)
 
         grouped, x_codes, x_planes = {}, {}, {}
+
+        def scalar_copy(out, in_):
+            nc.scalar.activation(out=out, in_=in_, func=COPY)
 
         def interleave(half, a, copy):
             name = "grouped%d%d" % (half, a)
@@ -162,28 +166,36 @@ def tile_list_interp_relu_kernel(
                 in_=grouped[half, a][:].rearrange("p j t -> p (j t)"),
             )
 
-        for half in range(2):
-            interleave(half, 0, nc.scalar.copy)
-            quantise(half, 0)
-        interleave(0, 1, nc.vector.tensor_copy)
-        quantise(0, 1)
+        interleave(0, 0, scalar_copy)
+        interleave(1, 0, nc.vector.tensor_copy)
+        quantise(0, 0)
+        quantise(1, 0)
 
-        first = keep.tile([P, TILES, N], F32, name="first", tag="x_raw10")
+        first = keep.tile([P, TILES, N], F32, name="first")
         mixed = keep.tile([P, TILES, N], F32, name="mixed")
         for jt in range(TILES):
-            nc.scalar.activation(out=first[:, jt, :], in_=acc[0, jt][:], func=COPY, scale=iw[:, jt, 0:1])
+            nc.scalar.activation(out=first[:, jt, :], in_=acc[0, jt][:], func=COPY, scale=iw[0][:, jt : jt + 1])
         for jt in range(TILES):
+            for a in range(PASSES):
+                table_pass(1, jt, a)
+        interleave(0, 1, scalar_copy)
+        interleave(1, 1, scalar_copy)
+
+        def mix(jt):
             nc.vector.scalar_tensor_tensor(
-                out=mixed[:, jt, :], in0=acc[1, jt][:], scalar=iw[:, jt, 1:2], in1=first[:, jt, :], op0=MULT, op1=ADD
+                out=mixed[:, jt, :],
+                in0=acc[1, jt][:],
+                scalar=iw[1][:, jt : jt + 1],
+                in1=first[:, jt, :],
+                op0=MULT,
+                op1=ADD,
             )
-        interleave(1, 1, nc.scalar.copy)
-        quantise(1, 1)
 
         skip = {}
 
         def skip_pass(jt, a):
             if a == 0:
-                skip[jt] = psum.tile([P, N], F32, name="skip%d" % jt, tag="bank")
+                skip[jt] = psum.tile([P, N], F32, name="skip%d" % jt, tag="bank%d" % jt)
             half, c = divmod(jt * P, HALF)
             nc.tensor.matmul_mx(
                 out=skip[jt][:],
@@ -195,16 +207,16 @@ def tile_list_interp_relu_kernel(
                 stop=(a == PASSES - 1),
             )
 
-        for half in range(2):
-            for a in range(PASSES):
-                for jt in (2 * half, 2 * half + 1):
-                    skip_pass(jt, a)
+        total = keep.tile([P, TILES, N], F32, name="total")
 
-        total = keep.tile([P, TILES, N], F32, name="total", tag="grouped11", align_bytes=64)
-        for jt in range(TILES):
+        def add_skip(jt):
             nc.vector.tensor_tensor(out=total[:, jt, :], in0=skip[jt][:], in1=mixed[:, jt, :], op=ADD)
-        for half in range(2):
-            turned = [psum.tile([P, 2, HALF], F32, name="turned%d%d" % (half, b), tag="bank") for b in range(2)]
+
+        def finish(half):
+            turned = [
+                psum.tile([P, 2, HALF], F32, name="turned%d%d" % (half, b), tag="bank%d" % (TILES + 2 * half + b))
+                for b in range(2)
+            ]
             for s in range(2):
                 for nt in range(N // P):
                     nc.tensor.transpose(
@@ -218,3 +230,15 @@ def tile_list_interp_relu_kernel(
                     nc.scalar.activation(out=result[:], in_=turned[b][:], func=RELU)
                 rows = out[2 * P * b : 2 * P * (b + 1), HALF * half : HALF * (half + 1)]
                 nc.sync.dma_start(out=rows.rearrange("(r p) j -> p r j", p=P), in_=result[:])
+
+        for half in range(2):
+            mix(2 * half)
+            mix(2 * half + 1)
+            quantise(half, 1)
+            for jt in (2 * half, 2 * half + 1):
+                for a in range(PASSES):
+                    skip_pass(jt, a)
+        for half in range(2):
+            add_skip(2 * half)
+            add_skip(2 * half + 1)
+            finish(half)

@@ -30,6 +30,8 @@ SECOND = 16
 LIST_ROWS = 16
 TILES = J // P
 HALF = J // 2
+AHEAD = T // 4
+EARLY = 5 * P
 
 
 def tile_list_interp_relu_kernel(
@@ -38,6 +40,7 @@ def tile_list_interp_relu_kernel(
     nc = tc.nc
     with ExitStack() as ctx:
         keep = ctx.enter_context(tc.tile_pool(name="keep", bufs=1))
+        shared = ctx.enter_context(tc.tile_pool(name="shared", bufs=1))
         psum = ctx.enter_context(tc.psum_pool(name="psum", bufs=1))
 
         offsets = keep.tile([P, LISTS * J // LIST_ROWS], U16, name="offsets")
@@ -47,12 +50,14 @@ def tile_list_interp_relu_kernel(
         w_codes = keep.tile([P, PASSES, N], I32, name="w_codes", align_bytes=64)
         wx_planes = keep.tile([P, PASSES, N], U8, name="wx_planes", align_bytes=64)
         wx_codes = keep.tile([P, PASSES, 2 * N], U8, name="wx_codes", align_bytes=64)
-        moved_planes = [keep.tile([P, J], U8, name="moved_plane%d" % g, align_bytes=64) for g in range(LISTS)]
+        parts = ((0, EARLY), (EARLY, LISTS * J - EARLY))
+        moved_planes = [keep.tile([P, count], U8, name="moved_plane%d" % first, align_bytes=64) for first, count in parts]
         iw = [keep.tile([P, TILES], F32, name="iw%d" % g) for g in range(LISTS)]
         ident = keep.tile([P, P], F32, name="ident")
 
         nc.vector.memset(tab_plane[:, 0 : T // 2].bitcast(I32), 0)
         nc.gpsimd.memset(tab_plane[:, T // 2 : T].bitcast(I32), 0)
+        make_identity(nc, ident[:])
         for planes in (w_planes, wx_planes):
             nc.vector.memset(planes[:].rearrange("p a n -> p (a n)").bitcast(I32), 0)
         for plane in moved_planes:
@@ -69,7 +74,8 @@ def tile_list_interp_relu_kernel(
 
         def load_x(a, halves):
             width = HALF * len(halves)
-            raw = keep.tile([P, PACK, width], F32, name="x_raw%d%d" % (halves[0], a))
+            name = "x_raw%d%d" % (halves[0], a)
+            raw = keep.tile([P, PACK, width], F32, name=name, tag=name, align_bytes=64)
             rows = x[K_PASS * a : K_PASS * (a + 1), HALF * halves[0] : HALF * halves[0] + width]
             nc.sync.dma_start(out=raw[:], in_=rows.rearrange("(p t) j -> p t j", t=PACK))
             for i, half in enumerate(halves):
@@ -77,31 +83,32 @@ def tile_list_interp_relu_kernel(
 
         nc.sync.dma_start(offsets[:], offs)
         tab_rows = tab_words[0].rearrange("p t b -> p (t b)").bitcast(I32)
-        nc.sync.dma_start(out=tab_codes[:, 0 : T // 2], in_=tab_rows[:, 0 : T // 2])
+        nc.sync.dma_start(out=tab_codes[:, 0:AHEAD], in_=tab_rows[:, 0:AHEAD])
         for r in range(SCALE_ROWS):
             nc.sync.dma_start(
                 out=tab_plane[r:P:SECOND, :].bitcast(I32),
                 in_=tab_scales[:, r : QUADS * SCALE_ROWS : SCALE_ROWS, :].rearrange("a q t -> q a t").bitcast(I32),
             )
-        nc.sync.dma_start(out=tab_codes[:, T // 2 : T], in_=tab_rows[:, T // 2 : T])
+        nc.sync.dma_start(out=tab_codes[:, AHEAD:T], in_=tab_rows[:, AHEAD:T])
         nc.sync.dma_start(out=w_codes[:], in_=w_words.rearrange("a p n b -> p a (n b)").bitcast(I32))
         load_planes(nc.sync, w_planes, w_scales)
-        load_x(0, (0, 1))
+        load_x(0, (0,))
         with nc.allow_non_contiguous_dma(reason="one weight a partition"):
             for g, weights in enumerate((iw0, iw1)):
                 nc.gpsimd.dma_start(out=iw[g][:], in_=weights.rearrange("(c p) -> p c", p=P))
         load_planes(nc.gpsimd, wx_planes, wx_scales)
-        make_identity(nc, ident[:])
 
         v_planes, v_codes = {}, {}
 
-        def gather_scales(g, tag):
-            picked = keep.tile([P, J], U8, name="picked_plane%d" % g, tag=tag, align_bytes=64)
-            columns = slice(g * J // LIST_ROWS, (g + 1) * J // LIST_ROWS)
+        def gather_scales(part, tag):
+            first, count = parts[part]
+            moved = moved_planes[part]
+            picked = keep.tile([P, count], U8, name="picked_plane%d" % first, tag=tag, align_bytes=64)
+            columns = slice(first // LIST_ROWS, (first + count) // LIST_ROWS)
             nc.vector.tensor_copy(picked[:], tab_plane[:].indirect(offsets[:, columns]))
-            nc.sync.dma_start(out=moved_planes[g][0 : P - SECOND, :].bitcast(I32), in_=picked[SECOND:P, :].bitcast(I32))
-            for jt in range(TILES):
-                v_planes[g, jt] = (picked[:, jt * P : (jt + 1) * P], moved_planes[g][:, jt * P : (jt + 1) * P])
+            nc.sync.dma_start(out=moved[0 : P - SECOND, :].bitcast(I32), in_=picked[SECOND:P, :].bitcast(I32))
+            for c in range(0, count, P):
+                v_planes[divmod((first + c) // P, TILES)] = (picked[:, c : c + P], moved[:, c : c + P])
 
         def gather_words(first, count, tag):
             words = keep.tile([P, count], U32, name="picked%d" % first, tag=tag, align_bytes=64)
@@ -111,25 +118,26 @@ def tile_list_interp_relu_kernel(
 
         def part_words(first, count, words, tag):
             parted = keep.tile([P, PASSES, count], U16, name="parted%d" % first, tag=tag, align_bytes=64)
-            nc.vector.tensor_copy(parted[:], words[:].bitcast(U16).rearrange("p (c a) -> p a c", a=PASSES))
+            nc.vector.tensor_copy(parted[:], words.bitcast(U16).rearrange("p (c a) -> p a c", a=PASSES))
             for c in range(0, count, P):
                 v_codes[divmod((first + c) // P, TILES)] = parted[:, :, c : c + P]
 
         gather_scales(0, "picked_plane")
+        load_x(0, (1,))
         load_x(1, (0,))
         words = [gather_words(HALF * half, HALF, "picked%d" % half) for half in range(2)]
-        part_words(0, HALF, words[0], "parted0")
+        part_words(0, HALF, words[0][:], "parted0")
+        part_words(HALF, HALF, words[1][:], "parted1")
         gather_scales(1, "picked0")
         nc.sync.dma_start(out=wx_codes[:].bitcast(I32), in_=wx_words.rearrange("a p n -> p a n").bitcast(I32))
         load_x(1, (1,))
-        part_words(HALF, HALF, words[1], "tab_plane")
-        part_words(J, J, gather_words(J, J, "picked1"), "parted2")
+        part_words(J, J, gather_words(J, J, "picked1")[:], "parted0")
 
         acc = {}
 
         def table_pass(g, jt, a):
             if a == 0:
-                acc[g, jt] = psum.tile([P, N], F32, name="acc%d%d" % (g, jt), tag="bank%d" % jt)
+                acc[g, jt] = psum.tile([P, N], F32, name="acc%d%d" % (g, jt), tag="bank%d" % (TILES * g + jt))
             nc.tensor.matmul_mx(
                 out=acc[g, jt][:],
                 lhsT=v_codes[g, jt][:, a, :].bitcast(FP4X4),
@@ -149,16 +157,16 @@ def tile_list_interp_relu_kernel(
         def scalar_copy(out, in_):
             nc.scalar.activation(out=out, in_=in_, func=COPY)
 
-        def interleave(half, a, copy):
+        def interleave(half, a, copy, pool=keep, offset=None):
             name = "grouped%d%d" % (half, a)
-            grouped[half, a] = keep.tile([P, HALF, PACK], BF16, name=name, tag=name, align_bytes=64)
+            grouped[half, a] = pool.tile([P, HALF, PACK], BF16, name=name, tag=name, align_bytes=64, offset=offset)
             copy(
                 out=grouped[half, a][:].rearrange("p (c i) t -> p c t i", i=4),
                 in_=x_raw[half, a].rearrange("p t (c i) -> p c t i", i=4),
             )
 
-        def quantise(half, a):
-            x_codes[half, a] = keep.tile([P, HALF], U32, name="x_codes%d%d" % (half, a), align_bytes=64)
+        def quantise(half, a, tag):
+            x_codes[half, a] = keep.tile([P, HALF], U32, name="x_codes%d%d" % (half, a), tag=tag, align_bytes=64)
             x_planes[half, a] = keep.tile([P, HALF], U8, name="x_plane%d%d" % (half, a), align_bytes=64)
             nc.vector.quantize_mx(
                 out=x_codes[half, a][:].bitcast(FP8X4),
@@ -167,26 +175,32 @@ def tile_list_interp_relu_kernel(
             )
 
         interleave(0, 0, scalar_copy)
-        interleave(1, 0, nc.vector.tensor_copy)
-        quantise(0, 0)
-        quantise(1, 0)
+        interleave(1, 0, scalar_copy)
+        quantise(0, 0, "x_codes00")
+        quantise(1, 0, "x_codes10")
+        interleave(0, 1, scalar_copy)
+        quantise(0, 1, "x_codes01")
 
-        first = keep.tile([P, TILES, N], F32, name="first")
-        mixed = keep.tile([P, TILES, N], F32, name="mixed")
+        first, mixed, total = {}, {}, {}
+        firsts = keep.tile([P, TILES, N], F32, name="firsts", tag="x_raw01", align_bytes=64)
         for jt in range(TILES):
-            nc.scalar.activation(out=first[:, jt, :], in_=acc[0, jt][:], func=COPY, scale=iw[0][:, jt : jt + 1])
+            first[jt] = firsts[:, jt, :]
+            nc.scalar.activation(out=first[jt], in_=acc[0, jt][:], func=COPY, scale=iw[0][:, jt : jt + 1])
         for jt in range(TILES):
             for a in range(PASSES):
                 table_pass(1, jt, a)
-        interleave(0, 1, scalar_copy)
-        interleave(1, 1, scalar_copy)
+        grouped[1, 1] = shared.tile([P, HALF, PACK], BF16, name="grouped11", align_bytes=64, offset=1024)
+        nc.gpsimd.tensor_scalar(
+            out=grouped[1, 1][:], in0=x_raw[1, 1].rearrange("p t j -> p j t"), scalar1=1.0, scalar2=0.0, op0=MULT, op1=ADD
+        )
 
-        def mix(jt):
+        def mix(jt, tile):
+            mixed[jt] = tile
             nc.vector.scalar_tensor_tensor(
-                out=mixed[:, jt, :],
+                out=mixed[jt][:],
                 in0=acc[1, jt][:],
                 scalar=iw[1][:, jt : jt + 1],
-                in1=first[:, jt, :],
+                in1=first[jt],
                 op0=MULT,
                 op1=ADD,
             )
@@ -207,38 +221,62 @@ def tile_list_interp_relu_kernel(
                 stop=(a == PASSES - 1),
             )
 
-        total = keep.tile([P, TILES, N], F32, name="total")
 
-        def add_skip(jt):
-            nc.vector.tensor_tensor(out=total[:, jt, :], in0=skip[jt][:], in1=mixed[:, jt, :], op=ADD)
+        def add_skip(jt, tile):
+            total[jt] = tile
+            if jt % 2 == 0:
+                nc.vector.tensor_tensor(out=total[jt][:], in0=skip[jt][:], in1=mixed[jt][:], op=ADD)
+            else:
+                nc.scalar.copy(out=total[jt][:], in_=skip[jt][:])
 
-        def finish(half):
+        def finish(half, banks, relus):
+            blocks = N // P // len(banks)
+            terms = [(mixed[2 * half + 1][:], 1), (total[2 * half + 1][:], 1), (total[2 * half][:], 0)]
             turned = [
-                psum.tile([P, 2, HALF], F32, name="turned%d%d" % (half, b), tag="bank%d" % (TILES + 2 * half + b))
-                for b in range(2)
+                psum.tile([P, blocks, HALF], F32, name="turned%d%d" % (half, b), tag="bank%d" % bank)
+                for b, bank in enumerate(banks)
             ]
-            for s in range(2):
-                for nt in range(N // P):
-                    nc.tensor.transpose(
-                        turned[nt // 2][:, nt % 2, s * P : (s + 1) * P], total[:, 2 * half + s, nt * P : (nt + 1) * P], ident[:]
+            steps = [(i, nt) for i in range(len(terms)) for nt in range(N // P)]
+            if blocks > 1:
+                steps = sorted(steps, key=lambda step: step[1] // blocks)
+            for i, nt in steps:
+                    term, s = terms[i]
+                    b, r = divmod(nt, blocks)
+                    nc.tensor.matmul(
+                        turned[b][:, r, s * P : (s + 1) * P],
+                        lhsT=term[:, nt * P : (nt + 1) * P],
+                        rhs=ident[:],
+                        is_transpose=True,
+                        start=(i == 0 and r == 0),
+                        stop=(i == len(terms) - 1 and r == blocks - 1),
                     )
-            for b in range(2):
-                result = keep.tile([P, 2, HALF], F32, name="result%d%d" % (half, b))
-                if (half, b) == (1, 1):
-                    nc.vector.tensor_scalar_max(result[:], turned[b][:], 0.0)
-                else:
-                    nc.scalar.activation(out=result[:], in_=turned[b][:], func=RELU)
-                rows = out[2 * P * b : 2 * P * (b + 1), HALF * half : HALF * (half + 1)]
+            for b in range(len(banks)):
+                result = keep.tile([P, blocks, HALF], F32, name="result%d%d" % (half, b))
+                relus[b % len(relus)](result[:], turned[b][:])
+                rows = out[blocks * P * b : blocks * P * (b + 1), HALF * half : HALF * (half + 1)]
                 nc.sync.dma_start(out=rows.rearrange("(r p) j -> p r j", p=P), in_=result[:])
 
+        def scalar_relu(result, bank):
+            nc.scalar.activation(out=result, in_=bank, func=RELU)
+
+        def vector_relu(result, bank):
+            nc.vector.tensor_scalar_max(result, bank, 0.0)
+
+        def sums(name, tag):
+            return keep.tile([P, N], F32, name=name, tag=tag, align_bytes=64)
+
+        mix(0, sums("mixed0", "mixed0"))
+        mix(1, sums("mixed1", "mixed1"))
+        mix(2, sums("mixed2", "mixed2"))
+        quantise(1, 1, "x_codes11")
         for half in range(2):
-            mix(2 * half)
-            mix(2 * half + 1)
-            quantise(half, 1)
-            for jt in (2 * half, 2 * half + 1):
-                for a in range(PASSES):
-                    skip_pass(jt, a)
-        for half in range(2):
-            add_skip(2 * half)
-            add_skip(2 * half + 1)
-            finish(half)
+            for a in range(PASSES):
+                skip_pass(2 * half, a)
+                skip_pass(2 * half + 1, a)
+        add_skip(0, shared.tile([P, N], F32, name="total0", align_bytes=64, offset=2048))
+        add_skip(1, sums("total1", "total1"))
+        mix(3, shared.tile([P, N], F32, name="mixed3", align_bytes=64, offset=0))
+        add_skip(3, sums("total3", "total3"))
+        add_skip(2, sums("total2", "total2"))
+        finish(0, (4, 5), (scalar_relu,))
+        finish(1, (0, 1, 6, 7), (vector_relu, scalar_relu))

@@ -52,12 +52,14 @@ def tile_list_interp_relu_kernel(
         wx_codes = keep.tile([P, PASSES, 2 * N], U8, name="wx_codes", align_bytes=64)
         parts = ((0, EARLY), (EARLY, LISTS * J - EARLY))
         moved_planes = [keep.tile([P, count], U8, name="moved_plane%d" % first, align_bytes=64) for first, count in parts]
-        iw = [keep.tile([P, TILES], F32, name="iw%d" % g) for g in range(LISTS)]
+        iw_rows = keep.tile([P, P], F32, name="iw_rows")
+        iw = keep.tile([P, LISTS * TILES], F32, name="iw")
         ident = keep.tile([P, P], F32, name="ident")
 
         nc.vector.memset(tab_plane[:, 0 : T // 2].bitcast(I32), 0)
         nc.gpsimd.memset(tab_plane[:, T // 2 : T].bitcast(I32), 0)
         make_identity(nc, ident[:])
+        nc.vector.memset(iw_rows[:], 0.0)
         for planes in (w_planes, wx_planes):
             nc.vector.memset(planes[:].rearrange("p a n -> p (a n)").bitcast(I32), 0)
         for plane in moved_planes:
@@ -93,9 +95,11 @@ def tile_list_interp_relu_kernel(
         nc.sync.dma_start(out=w_codes[:], in_=w_words.rearrange("a p n b -> p a (n b)").bitcast(I32))
         load_planes(nc.sync, w_planes, w_scales)
         load_x(0, (0,))
-        with nc.allow_non_contiguous_dma(reason="one weight a partition"):
-            for g, weights in enumerate((iw0, iw1)):
-                nc.gpsimd.dma_start(out=iw[g][:], in_=weights.rearrange("(c p) -> p c", p=P))
+        for g, weights in enumerate((iw0, iw1)):
+            nc.gpsimd.dma_start(out=iw_rows[TILES * g : TILES * (g + 1), :], in_=weights.rearrange("(c p) -> c p", p=P))
+        iw_turned = psum.tile([P, P], F32, name="iw_turned", tag="bank7")
+        nc.tensor.transpose(iw_turned[:], iw_rows[:], ident[:])
+        nc.scalar.activation(out=iw[:], in_=iw_turned[:, 0 : LISTS * TILES], func=COPY)
         load_planes(nc.gpsimd, wx_planes, wx_scales)
 
         v_planes, v_codes = {}, {}
@@ -185,7 +189,7 @@ def tile_list_interp_relu_kernel(
         firsts = keep.tile([P, TILES, N], F32, name="firsts", tag="x_raw01", align_bytes=64)
         for jt in range(TILES):
             first[jt] = firsts[:, jt, :]
-            nc.scalar.activation(out=first[jt], in_=acc[0, jt][:], func=COPY, scale=iw[0][:, jt : jt + 1])
+            nc.scalar.activation(out=first[jt], in_=acc[0, jt][:], func=COPY, scale=iw[:, jt : jt + 1])
         for jt in range(TILES):
             for a in range(PASSES):
                 table_pass(1, jt, a)
@@ -199,7 +203,7 @@ def tile_list_interp_relu_kernel(
             nc.vector.scalar_tensor_tensor(
                 out=mixed[jt][:],
                 in0=acc[1, jt][:],
-                scalar=iw[1][:, jt : jt + 1],
+                scalar=iw[:, TILES + jt : TILES + jt + 1],
                 in1=first[jt],
                 op0=MULT,
                 op1=ADD,

@@ -49,7 +49,7 @@ def tile_list_interp_relu_kernel(
         w_planes = keep.tile([P, PASSES, N], U8, name="w_planes", align_bytes=64)
         w_codes = keep.tile([P, PASSES, N], I32, name="w_codes", align_bytes=64)
         wx_planes = keep.tile([P, PASSES, N], U8, name="wx_planes", align_bytes=64)
-        wx_codes = keep.tile([P, PASSES, 2 * N], U8, name="wx_codes", align_bytes=64)
+        wx_codes = [keep.tile([P, 2 * N], U8, name="wx_codes%d" % a, align_bytes=64) for a in range(PASSES)]
         parts = ((0, EARLY), (EARLY, LISTS * J - EARLY))
         moved_planes = [keep.tile([P, count], U8, name="moved_plane%d" % first, align_bytes=64) for first, count in parts]
         iw_rows = keep.tile([P, P], F32, name="iw_rows")
@@ -58,8 +58,10 @@ def tile_list_interp_relu_kernel(
 
         nc.vector.memset(tab_plane[:, 0 : T // 2].bitcast(I32), 0)
         nc.gpsimd.memset(tab_plane[:, T // 2 : T].bitcast(I32), 0)
-        make_identity(nc, ident[:])
         nc.vector.memset(iw_rows[:], 0.0)
+        for g, weights in enumerate((iw0, iw1)):
+            nc.gpsimd.dma_start(out=iw_rows[TILES * g : TILES * (g + 1), :], in_=weights.rearrange("(c p) -> c p", p=P))
+        make_identity(nc, ident[:])
         for planes in (w_planes, wx_planes):
             nc.vector.memset(planes[:].rearrange("p a n -> p (a n)").bitcast(I32), 0)
         for plane in moved_planes:
@@ -95,8 +97,6 @@ def tile_list_interp_relu_kernel(
         nc.sync.dma_start(out=w_codes[:], in_=w_words.rearrange("a p n b -> p a (n b)").bitcast(I32))
         load_planes(nc.sync, w_planes, w_scales)
         load_x(0, (0,))
-        for g, weights in enumerate((iw0, iw1)):
-            nc.gpsimd.dma_start(out=iw_rows[TILES * g : TILES * (g + 1), :], in_=weights.rearrange("(c p) -> c p", p=P))
         iw_turned = psum.tile([P, P], F32, name="iw_turned", tag="bank7")
         nc.tensor.transpose(iw_turned[:], iw_rows[:], ident[:])
         nc.scalar.activation(out=iw[:], in_=iw_turned[:, 0 : LISTS * TILES], func=COPY)
@@ -130,11 +130,13 @@ def tile_list_interp_relu_kernel(
         load_x(0, (1,))
         load_x(1, (0,))
         words = [gather_words(HALF * half, HALF, "picked%d" % half) for half in range(2)]
-        part_words(0, HALF, words[0][:], "parted0")
+        part_words(0, P, words[0][:, 0:P], "parted0")
+        part_words(P, P, words[0][:, P:HALF], "parted128")
         part_words(HALF, HALF, words[1][:], "parted1")
         gather_scales(1, "picked0")
-        nc.sync.dma_start(out=wx_codes[:].bitcast(I32), in_=wx_words.rearrange("a p n -> p a n").bitcast(I32))
+        nc.sync.dma_start(out=wx_codes[0][:].bitcast(I32), in_=wx_words[0].bitcast(I32))
         load_x(1, (1,))
+        nc.sync.dma_start(out=wx_codes[1][:].bitcast(I32), in_=wx_words[1].bitcast(I32))
         part_words(J, J, gather_words(J, J, "picked1")[:], "parted0")
 
         acc = {}
@@ -181,15 +183,16 @@ def tile_list_interp_relu_kernel(
         interleave(0, 0, scalar_copy)
         interleave(1, 0, scalar_copy)
         quantise(0, 0, "x_codes00")
-        quantise(1, 0, "x_codes10")
-        interleave(0, 1, scalar_copy)
-        quantise(0, 1, "x_codes01")
+        quantise(1, 0, "picked1")
 
         first, mixed, total = {}, {}, {}
-        firsts = keep.tile([P, TILES, N], F32, name="firsts", tag="x_raw01", align_bytes=64)
-        for jt in range(TILES):
-            first[jt] = firsts[:, jt, :]
-            nc.scalar.activation(out=first[jt], in_=acc[0, jt][:], func=COPY, scale=iw[:, jt : jt + 1])
+        for half, tag in enumerate(("x_raw10", "x_raw01")):
+            firsts = keep.tile([P, 2, N], F32, name="firsts%d" % half, tag=tag, align_bytes=64)
+            for jt in (2 * half, 2 * half + 1):
+                first[jt] = firsts[:, jt % 2, :]
+                nc.scalar.activation(out=first[jt], in_=acc[0, jt][:], func=COPY, scale=iw[:, jt : jt + 1])
+            if half == 0:
+                interleave(0, 1, scalar_copy)
         for jt in range(TILES):
             for a in range(PASSES):
                 table_pass(1, jt, a)
@@ -213,13 +216,13 @@ def tile_list_interp_relu_kernel(
 
         def skip_pass(jt, a):
             if a == 0:
-                skip[jt] = psum.tile([P, N], F32, name="skip%d" % jt, tag="bank%d" % jt)
+                skip[jt] = psum.tile([P, N], F32, name="skip%d" % jt, tag="bank%d" % (jt if jt < 2 else jt + 2))
             half, c = divmod(jt * P, HALF)
             nc.tensor.matmul_mx(
                 out=skip[jt][:],
                 lhsT=x_codes[half, a][:, c : c + P].bitcast(FP8X4),
                 lhsT_scale=x_planes[half, a][:, c : c + P],
-                rhs=wx_codes[:, a, :].bitcast(FP4X4),
+                rhs=wx_codes[a][:].bitcast(FP4X4),
                 rhs_scale=wx_planes[:, a, :],
                 start=(a == 0),
                 stop=(a == PASSES - 1),
@@ -236,6 +239,8 @@ def tile_list_interp_relu_kernel(
         def finish(half, banks, relus):
             blocks = N // P // len(banks)
             terms = [(mixed[2 * half + 1][:], 1), (total[2 * half + 1][:], 1), (total[2 * half][:], 0)]
+            if half == 0:
+                terms = terms[::-1]
             turned = [
                 psum.tile([P, blocks, HALF], F32, name="turned%d%d" % (half, b), tag="bank%d" % bank)
                 for b, bank in enumerate(banks)
@@ -271,16 +276,16 @@ def tile_list_interp_relu_kernel(
 
         mix(0, sums("mixed0", "mixed0"))
         mix(1, sums("mixed1", "mixed1"))
+        quantise(0, 1, "x_codes01")
         mix(2, sums("mixed2", "mixed2"))
         quantise(1, 1, "x_codes11")
-        for half in range(2):
-            for a in range(PASSES):
-                skip_pass(2 * half, a)
-                skip_pass(2 * half + 1, a)
+        for a in range(PASSES):
+            for jt in range(TILES):
+                skip_pass(jt, a)
         add_skip(0, shared.tile([P, N], F32, name="total0", align_bytes=64, offset=2048))
         add_skip(1, sums("total1", "total1"))
         mix(3, shared.tile([P, N], F32, name="mixed3", align_bytes=64, offset=0))
         add_skip(3, sums("total3", "total3"))
         add_skip(2, sums("total2", "total2"))
-        finish(0, (4, 5), (scalar_relu,))
+        finish(0, (2, 3), (scalar_relu,))
         finish(1, (0, 1, 6, 7), (vector_relu, scalar_relu))

@@ -246,8 +246,7 @@ def tile_list_interp_relu_kernel(
                 for b, bank in enumerate(banks)
             ]
             steps = [(i, nt) for i in range(len(terms)) for nt in range(N // P)]
-            if blocks > 1:
-                steps = sorted(steps, key=lambda step: step[1] // blocks)
+            steps = sorted(steps, key=lambda step: -1 if half == 1 and step[0] == 0 else step[1])
             for i, nt in steps:
                     term, s = terms[i]
                     b, r = divmod(nt, blocks)
@@ -287,5 +286,5 @@ def tile_list_interp_relu_kernel(
         mix(3, shared.tile([P, N], F32, name="mixed3", align_bytes=64, offset=0))
         add_skip(3, sums("total3", "total3"))
         add_skip(2, sums("total2", "total2"))
-        finish(0, (2, 3), (scalar_relu,))
-        finish(1, (0, 1, 6, 7), (vector_relu, scalar_relu))
+        finish(0, (2, 3, 0, 1), (scalar_relu, scalar_relu, vector_relu, scalar_relu))
+        finish(1, (6, 7, 5, 4), (vector_relu, scalar_relu))

@@ -26,12 +26,11 @@ PASSES = K // K_PASS
 LISTS = 2
 QUADS = 4
 SCALE_ROWS = 4
-SECOND = 16
+TAB_ROWS = PASSES * QUADS * SCALE_ROWS
 LIST_ROWS = 16
 TILES = J // P
+EARLY = 6 * P
 HALF = J // 2
-AHEAD = T // 4
-EARLY = 5 * P
 
 
 def tile_list_interp_relu_kernel(
@@ -41,6 +40,7 @@ def tile_list_interp_relu_kernel(
     with ExitStack() as ctx:
         keep = ctx.enter_context(tc.tile_pool(name="keep", bufs=1))
         shared = ctx.enter_context(tc.tile_pool(name="shared", bufs=1))
+        landed = ctx.enter_context(tc.tile_pool(name="landed", bufs=1))
         psum = ctx.enter_context(tc.psum_pool(name="psum", bufs=1))
 
         offsets = keep.tile([P, LISTS * J // LIST_ROWS], U16, name="offsets")
@@ -49,23 +49,24 @@ def tile_list_interp_relu_kernel(
         w_planes = keep.tile([P, PASSES, N], U8, name="w_planes", align_bytes=64)
         w_codes = keep.tile([P, PASSES, N], I32, name="w_codes", align_bytes=64)
         wx_planes = keep.tile([P, PASSES, N], U8, name="wx_planes", align_bytes=64)
-        wx_codes = [keep.tile([P, 2 * N], U8, name="wx_codes%d" % a, align_bytes=64) for a in range(PASSES)]
+        wx_codes = keep.tile([P, PASSES, 2 * N], U8, name="wx_codes", align_bytes=64)
         parts = ((0, EARLY), (EARLY, LISTS * J - EARLY))
-        moved_planes = [keep.tile([P, count], U8, name="moved_plane%d" % first, align_bytes=64) for first, count in parts]
+        picked_rows = [keep.tile([P, count], U8, name="picked_rows%d" % first, align_bytes=64) for first, count in parts]
+        moved_rows = [keep.tile([P, PASSES, count], U8, name="moved_rows%d" % first, align_bytes=64) for first, count in parts]
         iw_rows = keep.tile([P, P], F32, name="iw_rows")
         iw = keep.tile([P, LISTS * TILES], F32, name="iw")
         ident = keep.tile([P, P], F32, name="ident")
 
-        nc.vector.memset(tab_plane[:, 0 : T // 2].bitcast(I32), 0)
-        nc.gpsimd.memset(tab_plane[:, T // 2 : T].bitcast(I32), 0)
+        nc.vector.memset(w_planes[:].rearrange("p a n -> p (a n)").bitcast(I32), 0)
         nc.vector.memset(iw_rows[:], 0.0)
+        nc.vector.memset(wx_planes[:].rearrange("p a n -> p (a n)").bitcast(I32), 0)
+        nc.vector.memset(tab_plane[TAB_ROWS:64, :].bitcast(I32), 0)
+        nc.vector.memset(tab_plane[64:P, :].bitcast(I32), 0)
+        for moved in moved_rows:
+            nc.gpsimd.memset(moved[:].rearrange("p a n -> p (a n)").bitcast(I32), 0)
         for g, weights in enumerate((iw0, iw1)):
             nc.gpsimd.dma_start(out=iw_rows[TILES * g : TILES * (g + 1), :], in_=weights.rearrange("(c p) -> c p", p=P))
         make_identity(nc, ident[:])
-        for planes in (w_planes, wx_planes):
-            nc.vector.memset(planes[:].rearrange("p a n -> p (a n)").bitcast(I32), 0)
-        for plane in moved_planes:
-            nc.vector.memset(plane[P - 32 : P, :].bitcast(I32), 0)
 
         def load_planes(queue, planes, scales):
             for quad in range(QUADS):
@@ -76,26 +77,20 @@ def tile_list_interp_relu_kernel(
 
         x_raw = {}
 
-        def load_x(a, halves):
+        def load_x(a, halves, pool=keep, offset=None):
             width = HALF * len(halves)
             name = "x_raw%d%d" % (halves[0], a)
-            raw = keep.tile([P, PACK, width], F32, name=name, tag=name, align_bytes=64)
+            raw = pool.tile([P, PACK, width], F32, name=name, tag=name, align_bytes=64, offset=offset)
             rows = x[K_PASS * a : K_PASS * (a + 1), HALF * halves[0] : HALF * halves[0] + width]
             nc.sync.dma_start(out=raw[:], in_=rows.rearrange("(p t) j -> p t j", t=PACK))
             for i, half in enumerate(halves):
                 x_raw[half, a] = raw[:, :, HALF * i : HALF * (i + 1)]
 
+        nc.sync.dma_start(out=tab_plane[0:TAB_ROWS, :].bitcast(I32), in_=tab_scales.rearrange("a q t -> q a t").bitcast(I32))
         nc.sync.dma_start(offsets[:], offs)
-        tab_rows = tab_words[0].rearrange("p t b -> p (t b)").bitcast(I32)
-        nc.sync.dma_start(out=tab_codes[:, 0:AHEAD], in_=tab_rows[:, 0:AHEAD])
-        for r in range(SCALE_ROWS):
-            nc.sync.dma_start(
-                out=tab_plane[r:P:SECOND, :].bitcast(I32),
-                in_=tab_scales[:, r : QUADS * SCALE_ROWS : SCALE_ROWS, :].rearrange("a q t -> q a t").bitcast(I32),
-            )
-        nc.sync.dma_start(out=tab_codes[:, AHEAD:T], in_=tab_rows[:, AHEAD:T])
-        nc.sync.dma_start(out=w_codes[:], in_=w_words.rearrange("a p n b -> p a (n b)").bitcast(I32))
+        nc.sync.dma_start(out=tab_codes[:], in_=tab_words[0].rearrange("p t b -> p (t b)").bitcast(I32))
         load_planes(nc.sync, w_planes, w_scales)
+        nc.sync.dma_start(out=w_codes[:], in_=w_words.rearrange("a p n b -> p a (n b)").bitcast(I32))
         load_x(0, (0,))
         iw_turned = psum.tile([P, P], F32, name="iw_turned", tag="bank7")
         nc.tensor.transpose(iw_turned[:], iw_rows[:], ident[:])
@@ -104,15 +99,19 @@ def tile_list_interp_relu_kernel(
 
         v_planes, v_codes = {}, {}
 
-        def gather_scales(part, tag):
-            first, count = parts[part]
-            moved = moved_planes[part]
-            picked = keep.tile([P, count], U8, name="picked_plane%d" % first, tag=tag, align_bytes=64)
+        for picked, (first, count) in zip(picked_rows, parts):
             columns = slice(first // LIST_ROWS, (first + count) // LIST_ROWS)
             nc.vector.tensor_copy(picked[:], tab_plane[:].indirect(offsets[:, columns]))
-            nc.sync.dma_start(out=moved[0 : P - SECOND, :].bitcast(I32), in_=picked[SECOND:P, :].bitcast(I32))
+
+        def move_rows(part):
+            first, count = parts[part]
+            for quad in range(QUADS):
+                nc.sync.dma_start(
+                    out=moved_rows[part][32 * quad : 32 * quad + SCALE_ROWS, :, :].bitcast(I32),
+                    in_=picked_rows[part][8 * quad : 8 * (quad + 1), :].bitcast(I32),
+                )
             for c in range(0, count, P):
-                v_planes[divmod((first + c) // P, TILES)] = (picked[:, c : c + P], moved[:, c : c + P])
+                v_planes[divmod((first + c) // P, TILES)] = moved_rows[part][:, :, c : c + P]
 
         def gather_words(first, count, tag):
             words = keep.tile([P, count], U32, name="picked%d" % first, tag=tag, align_bytes=64)
@@ -126,37 +125,47 @@ def tile_list_interp_relu_kernel(
             for c in range(0, count, P):
                 v_codes[divmod((first + c) // P, TILES)] = parted[:, :, c : c + P]
 
-        gather_scales(0, "picked_plane")
-        load_x(0, (1,))
+        move_rows(0)
+        load_x(0, (1,), landed, 2048)
         load_x(1, (0,))
-        words = [gather_words(HALF * half, HALF, "picked%d" % half) for half in range(2)]
-        part_words(0, P, words[0][:, 0:P], "parted0")
-        part_words(P, P, words[0][:, P:HALF], "parted128")
-        part_words(HALF, HALF, words[1][:], "parted1")
-        gather_scales(1, "picked0")
-        nc.sync.dma_start(out=wx_codes[0][:].bitcast(I32), in_=wx_words[0].bitcast(I32))
+        move_rows(1)
+        nc.sync.dma_start(out=wx_codes[:].bitcast(I32), in_=wx_words.rearrange("a p n -> p a n").bitcast(I32))
         load_x(1, (1,))
-        nc.sync.dma_start(out=wx_codes[1][:].bitcast(I32), in_=wx_words[1].bitcast(I32))
-        part_words(J, J, gather_words(J, J, "picked1")[:], "parted0")
+        words = [gather_words(HALF * half, HALF, "picked%d" % half) for half in range(2)]
+        for half in range(2):
+            part_words(HALF * half, HALF, words[half][:], "parted%d" % half)
+        part_words(J, J, gather_words(J, J, "picked1")[:], "parted2")
+
+        unread = psum.tile([P, N], F32, name="unread", tag="bank6")
+        for a in range(PASSES):
+            nc.tensor.matmul_mx(
+                out=unread[:],
+                lhsT=words[0][:, 0 : P // 2].bitcast(FP4X4),
+                lhsT_scale=picked_rows[0][:, 0:P],
+                rhs=w_codes[:, a, :].bitcast(FP8X4),
+                rhs_scale=w_planes[:, a, :],
+                start=True,
+                stop=True,
+            )
 
         acc = {}
 
-        def table_pass(g, jt, a):
-            if a == 0:
+        def table_pass(g, jt, a, opens):
+            if opens:
                 acc[g, jt] = psum.tile([P, N], F32, name="acc%d%d" % (g, jt), tag="bank%d" % (TILES * g + jt))
             nc.tensor.matmul_mx(
                 out=acc[g, jt][:],
                 lhsT=v_codes[g, jt][:, a, :].bitcast(FP4X4),
-                lhsT_scale=v_planes[g, jt][a],
+                lhsT_scale=v_planes[g, jt][:, a, :],
                 rhs=w_codes[:, a, :].bitcast(FP8X4),
                 rhs_scale=w_planes[:, a, :],
-                start=(a == 0),
-                stop=(a == PASSES - 1),
+                start=opens,
+                stop=not opens,
             )
 
-        for a in range(PASSES):
-            for jt in range(TILES):
-                table_pass(0, jt, a)
+        for jt in range(TILES):
+            for a in range(PASSES):
+                table_pass(0, jt, a, a == 0)
 
         grouped, x_codes, x_planes = {}, {}, {}
 
@@ -183,19 +192,17 @@ def tile_list_interp_relu_kernel(
         interleave(0, 0, scalar_copy)
         interleave(1, 0, scalar_copy)
         quantise(0, 0, "x_codes00")
-        quantise(1, 0, "picked1")
+        quantise(1, 0, "x_codes10")
 
         first, mixed, total = {}, {}, {}
-        for half, tag in enumerate(("x_raw10", "x_raw01")):
-            firsts = keep.tile([P, 2, N], F32, name="firsts%d" % half, tag=tag, align_bytes=64)
-            for jt in (2 * half, 2 * half + 1):
-                first[jt] = firsts[:, jt % 2, :]
-                nc.scalar.activation(out=first[jt], in_=acc[0, jt][:], func=COPY, scale=iw[:, jt : jt + 1])
-            if half == 0:
-                interleave(0, 1, scalar_copy)
+        for jt, offset in enumerate((64, 2048 + 64, 4096 + 64, 8192)):
+            first[jt] = landed.tile([P, N], F32, name="first%d" % jt, align_bytes=64, offset=offset)[:]
+            nc.scalar.activation(out=first[jt], in_=acc[0, jt][:], func=COPY, scale=iw[:, jt : jt + 1])
+        interleave(0, 1, nc.vector.tensor_copy, shared, 3072 - 64)
+        quantise(0, 1, "x_codes01")
         for jt in range(TILES):
             for a in range(PASSES):
-                table_pass(1, jt, a)
+                table_pass(1, jt, a, a == 0)
         grouped[1, 1] = shared.tile([P, HALF, PACK], BF16, name="grouped11", align_bytes=64, offset=1024)
         nc.gpsimd.tensor_scalar(
             out=grouped[1, 1][:], in0=x_raw[1, 1].rearrange("p t j -> p j t"), scalar1=1.0, scalar2=0.0, op0=MULT, op1=ADD
@@ -222,7 +229,7 @@ def tile_list_interp_relu_kernel(
                 out=skip[jt][:],
                 lhsT=x_codes[half, a][:, c : c + P].bitcast(FP8X4),
                 lhsT_scale=x_planes[half, a][:, c : c + P],
-                rhs=wx_codes[a][:].bitcast(FP4X4),
+                rhs=wx_codes[:, a, :].bitcast(FP4X4),
                 rhs_scale=wx_planes[:, a, :],
                 start=(a == 0),
                 stop=(a == PASSES - 1),
@@ -275,11 +282,10 @@ def tile_list_interp_relu_kernel(
 
         mix(0, sums("mixed0", "mixed0"))
         mix(1, sums("mixed1", "mixed1"))
-        quantise(0, 1, "x_codes01")
         mix(2, sums("mixed2", "mixed2"))
         quantise(1, 1, "x_codes11")
-        for a in range(PASSES):
-            for jt in range(TILES):
+        for jt in range(TILES):
+            for a in range(PASSES):
                 skip_pass(jt, a)
         add_skip(0, shared.tile([P, N], F32, name="total0", align_bytes=64, offset=2048))
         add_skip(1, sums("total1", "total1"))

@@ -130,7 +130,7 @@ def tile_list_interp_relu_kernel(
         load_x(1, (0,))
         move_rows(1)
         nc.sync.dma_start(out=wx_codes[:].bitcast(I32), in_=wx_words.rearrange("a p n -> p a n").bitcast(I32))
-        load_x(1, (1,))
+        load_x(1, (1,), landed, 12288)
         words = [gather_words(HALF * half, HALF, "picked%d" % half) for half in range(2)]
         for half in range(2):
             part_words(HALF * half, HALF, words[half][:], "parted%d" % half)
@@ -195,9 +195,13 @@ def tile_list_interp_relu_kernel(
         quantise(1, 0, "x_codes10")
 
         first, mixed, total = {}, {}, {}
-        for jt, offset in enumerate((64, 2048 + 64, 4096 + 64, 8192)):
+
+        def scale_first(jt, offset):
             first[jt] = landed.tile([P, N], F32, name="first%d" % jt, align_bytes=64, offset=offset)[:]
             nc.scalar.activation(out=first[jt], in_=acc[0, jt][:], func=COPY, scale=iw[:, jt : jt + 1])
+
+        for jt in range(3):
+            scale_first(jt, 64 + 2048 * jt)
         interleave(0, 1, nc.vector.tensor_copy, shared, 3072 - 64)
         quantise(0, 1, "x_codes01")
         for jt in range(TILES):
@@ -205,8 +209,18 @@ def tile_list_interp_relu_kernel(
                 table_pass(1, jt, a, a == 0)
         grouped[1, 1] = shared.tile([P, HALF, PACK], BF16, name="grouped11", align_bytes=64, offset=1024)
         nc.gpsimd.tensor_scalar(
-            out=grouped[1, 1][:], in0=x_raw[1, 1].rearrange("p t j -> p j t"), scalar1=1.0, scalar2=0.0, op0=MULT, op1=ADD
+            out=grouped[1, 1][:, 0:P, :],
+            in0=x_raw[1, 1][:, :, 0:P].rearrange("p t j -> p j t"),
+            scalar1=1.0,
+            scalar2=0.0,
+            op0=MULT,
+            op1=ADD,
         )
+        scalar_copy(
+            out=grouped[1, 1][:, P:HALF, :].rearrange("p (c i) t -> p c t i", i=4),
+            in_=x_raw[1, 1][:, :, P:HALF].rearrange("p t (c i) -> p c t i", i=4),
+        )
+        scale_first(3, 12288)
 
         def mix(jt, tile):
             mixed[jt] = tile
@@ -288,7 +302,7 @@ def tile_list_interp_relu_kernel(
             for a in range(PASSES):
                 skip_pass(jt, a)
         add_skip(0, shared.tile([P, N], F32, name="total0", align_bytes=64, offset=2048))
-        add_skip(1, sums("total1", "total1"))
+        add_skip(1, landed.tile([P, N], F32, name="total1", align_bytes=64, offset=14336))
         mix(3, shared.tile([P, N], F32, name="mixed3", align_bytes=64, offset=0))
         add_skip(3, sums("total3", "total3"))
         add_skip(2, sums("total2", "total2"))

from contextlib import ExitStack

import concourse.mybir as mybir
from concourse.masks import make_identity

K, L, N, T, J = 1024, 1024, 512, 2048, 512
FLOPS = 2 * (2 * K + L) * N * J

F32 = mybir.dt.float32
BF16 = mybir.dt.bfloat16
I32 = mybir.dt.int32
U32 = mybir.dt.uint32
U16 = mybir.dt.uint16
U8 = mybir.dt.uint8
FP8X4 = mybir.dt.float8_e4m3fn_x4
FP4X4 = mybir.dt.float4_e2m1fn_x4
MULT = mybir.AluOpType.mult
ADD = mybir.AluOpType.add
COPY = mybir.ActivationFunctionType.Copy
RELU = mybir.ActivationFunctionType.Relu

P = 128
PACK = 4
K_PASS = P * PACK
PASSES = K // K_PASS
LISTS = 2
QUADS = 4
SCALE_ROWS = 4
TAB_ROWS = PASSES * QUADS * SCALE_ROWS
LIST_ROWS = 16
TILES = J // P
EARLY = 6 * P
HALF = J // 2


def tile_list_interp_relu_kernel(
    tc, tab_words, tab_scales, w_words, w_scales, x, wx_words, wx_scales, iw0, iw1, offs, out
):
    nc = tc.nc
    with ExitStack() as ctx:
        keep = ctx.enter_context(tc.tile_pool(name="keep", bufs=1))
        shared = ctx.enter_context(tc.tile_pool(name="shared", bufs=1))
        landed = ctx.enter_context(tc.tile_pool(name="landed", bufs=1))
        psum = ctx.enter_context(tc.psum_pool(name="psum", bufs=1))

        offsets = keep.tile([P, LISTS * J // LIST_ROWS], U16, name="offsets")
        tab_plane = keep.tile([P, T], U8, name="tab_plane", tag="tab_plane", align_bytes=64)
        tab_codes = keep.tile([P, T], I32, name="tab_codes", align_bytes=64)
        w_planes = keep.tile([P, PASSES, N], U8, name="w_planes", align_bytes=64)
        w_codes = keep.tile([P, PASSES, N], I32, name="w_codes", align_bytes=64)
        wx_planes = keep.tile([P, PASSES, N], U8, name="wx_planes", align_bytes=64)
        wx_codes = keep.tile([P, PASSES, 2 * N], U8, name="wx_codes", align_bytes=64)
        parts = ((0, EARLY), (EARLY, LISTS * J - EARLY))
        picked_rows = [keep.tile([P, count], U8, name="picked_rows%d" % first, align_bytes=64) for first, count in parts]
        moved_rows = [keep.tile([P, PASSES, count], U8, name="moved_rows%d" % first, align_bytes=64) for first, count in parts]
        iw_rows = keep.tile([P, P], F32, name="iw_rows")
        iw = keep.tile([P, LISTS * TILES], F32, name="iw")
        ident = keep.tile([P, P], F32, name="ident")

        nc.vector.memset(w_planes[:].rearrange("p a n -> p (a n)").bitcast(I32), 0)
        nc.vector.memset(iw_rows[:], 0.0)
        nc.vector.memset(wx_planes[:].rearrange("p a n -> p (a n)").bitcast(I32), 0)
        nc.vector.memset(tab_plane[TAB_ROWS:64, :].bitcast(I32), 0)
        nc.vector.memset(tab_plane[64:P, :].bitcast(I32), 0)
        for moved in moved_rows:
            nc.gpsimd.memset(moved[:].rearrange("p a n -> p (a n)").bitcast(I32), 0)
        for g, weights in enumerate((iw0, iw1)):
            nc.gpsimd.dma_start(out=iw_rows[TILES * g : TILES * (g + 1), :], in_=weights.rearrange("(c p) -> c p", p=P))
        make_identity(nc, ident[:])

        def load_planes(queue, planes, scales):
            for quad in range(QUADS):
                queue.dma_start(
                    out=planes[32 * quad : 32 * quad + SCALE_ROWS, :, :].bitcast(I32),
                    in_=scales[:, SCALE_ROWS * quad : SCALE_ROWS * (quad + 1), :].rearrange("a r n -> r a n").bitcast(I32),
                )

        x_raw = {}

        def load_x(a, halves, pool=keep, offset=None):
            width = HALF * len(halves)
            name = "x_raw%d%d" % (halves[0], a)
            raw = pool.tile([P, PACK, width], F32, name=name, tag=name, align_bytes=64, offset=offset)
            rows = x[K_PASS * a : K_PASS * (a + 1), HALF * halves[0] : HALF * halves[0] + width]
            nc.sync.dma_start(out=raw[:], in_=rows.rearrange("(p t) j -> p t j", t=PACK))
            for i, half in enumerate(halves):
                x_raw[half, a] = raw[:, :, HALF * i : HALF * (i + 1)]

        nc.sync.dma_start(out=tab_plane[0:TAB_ROWS, :].bitcast(I32), in_=tab_scales.rearrange("a q t -> q a t").bitcast(I32))
        nc.sync.dma_start(offsets[:], offs)
        nc.sync.dma_start(out=tab_codes[:], in_=tab_words[0].rearrange("p t b -> p (t b)").bitcast(I32))
        load_planes(nc.sync, w_planes, w_scales)
        nc.sync.dma_start(out=w_codes[:], in_=w_words.rearrange("a p n b -> p a (n b)").bitcast(I32))
        load_x(0, (0,))
        iw_turned = psum.tile([P, P], F32, name="iw_turned", tag="bank7")
        nc.tensor.transpose(iw_turned[:], iw_rows[:], ident[:])
        nc.scalar.activation(out=iw[:], in_=iw_turned[:, 0 : LISTS * TILES], func=COPY)
        load_planes(nc.gpsimd, wx_planes, wx_scales)

        v_planes, v_codes = {}, {}

        for picked, (first, count) in zip(picked_rows, parts):
            columns = slice(first // LIST_ROWS, (first + count) // LIST_ROWS)
            nc.vector.tensor_copy(picked[:], tab_plane[:].indirect(offsets[:, columns]))

        def move_rows(part):
            first, count = parts[part]
            for quad in range(QUADS):
                nc.sync.dma_start(
                    out=moved_rows[part][32 * quad : 32 * quad + SCALE_ROWS, :, :].bitcast(I32),
                    in_=picked_rows[part][8 * quad : 8 * (quad + 1), :].bitcast(I32),
                )
            for c in range(0, count, P):
                v_planes[divmod((first + c) // P, TILES)] = moved_rows[part][:, :, c : c + P]

        def gather_words(first, count, tag):
            words = keep.tile([P, count], U32, name="picked%d" % first, tag=tag, align_bytes=64)
            columns = slice(first // LIST_ROWS, (first + count) // LIST_ROWS)
            nc.vector.tensor_copy(words[:], tab_codes[:].bitcast(U32).indirect(offsets[:, columns]))
            return words

        def part_words(first, count, words, tag):
            parted = keep.tile([P, PASSES, count], U16, name="parted%d" % first, tag=tag, align_bytes=64)
            nc.vector.tensor_copy(parted[:], words.bitcast(U16).rearrange("p (c a) -> p a c", a=PASSES))
            for c in range(0, count, P):
                v_codes[divmod((first + c) // P, TILES)] = parted[:, :, c : c + P]

        move_rows(0)
        load_x(0, (1,), landed, 2048)
        load_x(1, (0,))
        move_rows(1)
        nc.sync.dma_start(out=wx_codes[:].bitcast(I32), in_=wx_words.rearrange("a p n -> p a n").bitcast(I32))
        load_x(1, (1,), landed, 12288)
        words = [gather_words(HALF * half, HALF, "picked%d" % half) for half in range(2)]
        for half in range(2):
            part_words(HALF * half, HALF, words[half][:], "parted%d" % half)
        part_words(J, J, gather_words(J, J, "picked1")[:], "parted2")

        unread = psum.tile([P, N], F32, name="unread", tag="bank6")
        for a in range(PASSES):
            nc.tensor.matmul_mx(
                out=unread[:],
                lhsT=words[0][:, 0 : P // 2].bitcast(FP4X4),
                lhsT_scale=picked_rows[0][:, 0:P],
                rhs=w_codes[:, a, :].bitcast(FP8X4),
                rhs_scale=w_planes[:, a, :],
                start=True,
                stop=True,
            )

        acc = {}

        def table_pass(g, jt, a, opens):
            if opens:
                acc[g, jt] = psum.tile([P, N], F32, name="acc%d%d" % (g, jt), tag="bank%d" % (TILES * g + jt))
            nc.tensor.matmul_mx(
                out=acc[g, jt][:],
                lhsT=v_codes[g, jt][:, a, :].bitcast(FP4X4),
                lhsT_scale=v_planes[g, jt][:, a, :],
                rhs=w_codes[:, a, :].bitcast(FP8X4),
                rhs_scale=w_planes[:, a, :],
                start=opens,
                stop=not opens,
            )

        for jt in range(TILES):
            for a in range(PASSES):
                table_pass(0, jt, a, a == 0)

        grouped, x_codes, x_planes = {}, {}, {}

        def scalar_copy(out, in_):
            nc.scalar.activation(out=out, in_=in_, func=COPY)

        def interleave(half, a, copy, pool=keep, offset=None):
            name = "grouped%d%d" % (half, a)
            grouped[half, a] = pool.tile([P, HALF, PACK], BF16, name=name, tag=name, align_bytes=64, offset=offset)
            copy(
                out=grouped[half, a][:].rearrange("p (c i) t -> p c t i", i=4),
                in_=x_raw[half, a].rearrange("p t (c i) -> p c t i", i=4),
            )

        def quantise(half, a, tag):
            x_codes[half, a] = keep.tile([P, HALF], U32, name="x_codes%d%d" % (half, a), tag=tag, align_bytes=64)
            x_planes[half, a] = keep.tile([P, HALF], U8, name="x_plane%d%d" % (half, a), align_bytes=64)
            nc.vector.quantize_mx(
                out=x_codes[half, a][:].bitcast(FP8X4),
                scales=x_planes[half, a][:],
                in_=grouped[half, a][:].rearrange("p j t -> p (j t)"),
            )

        interleave(0, 0, scalar_copy)
        interleave(1, 0, scalar_copy)
        quantise(0, 0, "x_codes00")
        quantise(1, 0, "x_codes10")

        first, mixed, total = {}, {}, {}

        def scale_first(jt, offset):
            first[jt] = landed.tile([P, N], F32, name="first%d" % jt, align_bytes=64, offset=offset)[:]
            nc.scalar.activation(out=first[jt], in_=acc[0, jt][:], func=COPY, scale=iw[:, jt : jt + 1])

        for jt in range(3):
            scale_first(jt, 64 + 2048 * jt)
        interleave(0, 1, nc.vector.tensor_copy, shared, 3072 - 64)
        quantise(0, 1, "x_codes01")
        for jt in range(TILES):
            for a in range(PASSES):
                table_pass(1, jt, a, a == 0)
        grouped[1, 1] = shared.tile([P, HALF, PACK], BF16, name="grouped11", align_bytes=64, offset=1024)
        nc.gpsimd.tensor_scalar(
            out=grouped[1, 1][:, 0:P, :],
            in0=x_raw[1, 1][:, :, 0:P].rearrange("p t j -> p j t"),
            scalar1=1.0,
            scalar2=0.0,
            op0=MULT,
            op1=ADD,
        )
        scalar_copy(
            out=grouped[1, 1][:, P:HALF, :].rearrange("p (c i) t -> p c t i", i=4),
            in_=x_raw[1, 1][:, :, P:HALF].rearrange("p t (c i) -> p c t i", i=4),
        )
        scale_first(3, 12288)

        def mix(jt, tile):
            mixed[jt] = tile
            nc.vector.scalar_tensor_tensor(
                out=mixed[jt][:],
                in0=acc[1, jt][:],
                scalar=iw[:, TILES + jt : TILES + jt + 1],
                in1=first[jt],
                op0=MULT,
                op1=ADD,
            )

        skip = {}

        def skip_pass(jt, a):
            if a == 0:
                skip[jt] = psum.tile([P, N], F32, name="skip%d" % jt, tag="bank%d" % (jt if jt < 2 else jt + 2))
            half, c = divmod(jt * P, HALF)
            nc.tensor.matmul_mx(
                out=skip[jt][:],
                lhsT=x_codes[half, a][:, c : c + P].bitcast(FP8X4),
                lhsT_scale=x_planes[half, a][:, c : c + P],
                rhs=wx_codes[:, a, :].bitcast(FP4X4),
                rhs_scale=wx_planes[:, a, :],
                start=(a == 0),
                stop=(a == PASSES - 1),
            )


        def add_skip(jt, tile):
            total[jt] = tile
            if jt % 2 == 0:
                nc.vector.tensor_tensor(out=total[jt][:], in0=skip[jt][:], in1=mixed[jt][:], op=ADD)
            else:
                nc.scalar.copy(out=total[jt][:], in_=skip[jt][:])

        def finish(half, banks, relus):
            blocks = N // P // len(banks)
            terms = [(mixed[2 * half + 1][:], 1), (total[2 * half + 1][:], 1), (total[2 * half][:], 0)]
            if half == 0:
                terms = terms[::-1]
            turned = [
                psum.tile([P, blocks, HALF], F32, name="turned%d%d" % (half, b), tag="bank%d" % bank)
                for b, bank in enumerate(banks)
            ]
            steps = [(i, nt) for i in range(len(terms)) for nt in range(N // P)]
            steps = sorted(steps, key=lambda step: -1 if half == 1 and step[0] == 0 else step[1])
            for i, nt in steps:
                    term, s = terms[i]
                    b, r = divmod(nt, blocks)
                    nc.tensor.matmul(
                        turned[b][:, r, s * P : (s + 1) * P],
                        lhsT=term[:, nt * P : (nt + 1) * P],
                        rhs=ident[:],
                        is_transpose=True,
                        start=(i == 0 and r == 0),
                        stop=(i == len(terms) - 1 and r == blocks - 1),
                    )
            for b in range(len(banks)):
                result = keep.tile([P, blocks, HALF], F32, name="result%d%d" % (half, b))
                relus[b % len(relus)](result[:], turned[b][:])
                rows = out[blocks * P * b : blocks * P * (b + 1), HALF * half : HALF * (half + 1)]
                nc.sync.dma_start(out=rows.rearrange("(r p) j -> p r j", p=P), in_=result[:])

        def scalar_relu(result, bank):
            nc.scalar.activation(out=result, in_=bank, func=RELU)

        def vector_relu(result, bank):
            nc.vector.tensor_scalar_max(result, bank, 0.0)

        def sums(name, tag):
            return keep.tile([P, N], F32, name=name, tag=tag, align_bytes=64)

        mix(0, sums("mixed0", "mixed0"))
        mix(1, sums("mixed1", "mixed1"))
        mix(2, sums("mixed2", "mixed2"))
        quantise(1, 1, "x_codes11")
        for jt in range(TILES):
            for a in range(PASSES):
                skip_pass(jt, a)
        add_skip(0, shared.tile([P, N], F32, name="total0", align_bytes=64, offset=2048))
        add_skip(1, landed.tile([P, N], F32, name="total1", align_bytes=64, offset=14336))
        mix(3, shared.tile([P, N], F32, name="mixed3", align_bytes=64, offset=0))
        add_skip(3, sums("total3", "total3"))
        add_skip(2, sums("total2", "total2"))
        finish(0, (2, 3, 0, 1), (scalar_relu, scalar_relu, vector_relu, scalar_relu))
        finish(1, (6, 7, 5, 4), (vector_relu, scalar_relu))
